import numpy as np
import ml_dtypes


def mxq(x, axis, fmt="e4m3"):
    dtype, down = {"e4m3": (ml_dtypes.float8_e4m3fn, 7), "e5m2": (ml_dtypes.float8_e5m2, 14)}[fmt]
    v = np.moveaxis(np.asarray(x, np.float32).astype(ml_dtypes.bfloat16).astype(np.float64), axis, -1)
    blocks = v.reshape(v.shape[:-1] + (-1, 32))
    amax = np.abs(blocks).max(-1, keepdims=True)
    byte = np.maximum(np.where(amax > 0, np.frexp(amax)[1] - 1 + 127, 0) - down, 1)
    scale = np.exp2(byte - 127.0)
    codes = (blocks / scale).astype(np.float32).astype(dtype).astype(np.float64)
    return np.moveaxis((codes * scale).reshape(v.shape), -1, axis)


WIDE = False


def mx_kscale(k):
    if not WIDE:
        return np.ones(k)
    levels = np.array([10, -10, 5, -5, 0])
    if k % 512:
        return np.exp2(np.random.permutation(np.resize(levels, k // 32))).repeat(32)
    a = np.empty((k // 512, 16))
    for p in range(k // 512):
        a[p, :8] = np.random.permutation(np.resize(levels, 8))
        for g in range(8):
            far = levels[np.abs(levels - a[p, g]) >= 10]
            a[p, g + 8] = far[np.random.randint(len(far))]
    return np.exp2(a.ravel()).repeat(32)


def f64(x):
    return np.asarray(x).astype(np.float64)


def striped(idx):
    return np.tile(np.asarray(idx).reshape(-1, 16).T, (8, 1)).astype(np.uint16)


def unstriped(offs):
    return offs[:16].T.reshape(-1).astype(np.int64)


E2M1 = np.array([0.0, 0.5, 1.0, 1.5, 2.0, 3.0, 4.0, 6.0, -0.0, -0.5, -1.0, -1.5, -2.0, -3.0, -4.0, -6.0])


def pack_weight(w, fmt):
    k, n = w.shape
    w = f64(np.asarray(w, np.float32).astype(ml_dtypes.bfloat16)).reshape(k // 32, 32, n)
    amax = np.abs(w).max(1)
    if fmt == "e4m3":
        byte = np.frexp(amax)[1] - 1 + 127 - 7
    else:
        mant, ex = np.frexp(amax / 6.0)
        byte = np.where(mant > 0.5, ex, ex - 1) + 127
    byte = np.clip(np.where(amax > 0, byte, 1), 1, 254)
    scaled = (w * np.exp2(127.0 - byte)[:, None, :]).reshape(k, n).astype(np.float32)
    by_word = np.ascontiguousarray(scaled.reshape(k // 512, 128, 4, n).transpose(0, 1, 3, 2))
    if fmt == "e4m3":
        words = by_word.astype(ml_dtypes.float8_e4m3fn).view(np.uint8)
    else:
        c = by_word.astype(ml_dtypes.float4_e2m1fn).view(np.uint8) & 0xF
        words = (c[..., 0::2] | (c[..., 1::2] << 4)).reshape(k // 512, 128, 2 * n)
    return np.ascontiguousarray(words), np.ascontiguousarray(byte.astype(np.uint8).reshape(k // 512, 16, n))


def unpack_weight(words, scales, fmt):
    g, _, n = scales.shape
    words = np.ascontiguousarray(words).reshape(g, 128, n, -1)
    if fmt == "e4m3":
        vals = words.view(ml_dtypes.float8_e4m3fn).astype(np.float64)
    else:
        nib = np.empty((g, 128, n, 4), np.uint8)
        nib[..., 0::2] = words & 0xF
        nib[..., 1::2] = words >> 4
        vals = E2M1[nib]
    vals = vals * np.repeat(np.exp2(scales.astype(np.float64) - 127.0), 8, axis=1)[..., None]
    return vals.transpose(0, 1, 3, 2).reshape(g * 512, n)


B, N, T, D, DV, NQ = 2, 1024, 4096, 512, 256, 256
PAGE = 512


def setup_inputs():
    n = np.random.standard_normal
    pages = np.random.permutation(T // PAGE)[:B * N // PAGE]
    idx = (pages[:, None] * PAGE + np.arange(PAGE)[None, :]).reshape(-1)
    s = mx_kscale(D)[:, None]
    u = np.ones(T)
    u[idx] = mx_kscale(B * N)
    r = np.random.uniform(0.5, 2.0, T)
    k = n((D, T)) / s
    v = n((DV, T)) / (u * r)
    kp = pack_weight(k, "e4m3")
    vp = pack_weight(v.T, "e4m3")
    return {
        "qT": (n((B, D, NQ)) * s * (1.30 / np.sqrt(D))).astype(np.float32),
        "k_words": kp[0],
        "k_scales": kp[1],
        "v_words": vp[0],
        "v_scales": vp[1],
        "vs": np.tile(u * r, (128, 1)).astype(np.float32),
        "sink": (2.0 + 3.0 * n((B, NQ, 1))).astype(np.float32),
        "offs": striped(idx),
        "voffs": striped((pages[:, None] * DV + np.arange(DV)[None, :]).reshape(-1)),
    }


def reference(qT, k_words, k_scales, v_words, v_scales, vs, sink, offs, voffs):
    idx = unstriped(offs)
    k = unpack_weight(k_words, k_scales, "e4m3")
    v = unpack_weight(v_words, v_scales, "e4m3")
    v = v.reshape(T // 512, 512, DV)[unstriped(voffs)[::DV] // DV].reshape(B, N, DV)
    pick = lambda x: x[:, idx].reshape(x.shape[0], B, N).transpose(1, 0, 2)
    q = f64(qT)
    score = mxq(q, 1, "e4m3").transpose(0, 2, 1) @ pick(k)
    m = np.maximum(score.max(-1, keepdims=True), f64(sink))
    p = np.exp(score - m)
    total = p.sum(-1, keepdims=True) + np.exp(f64(sink) - m)
    w = p * pick(f64(vs))[:, :1, :]
    y = mxq(w, 2, "e4m3") @ v
    y = y / total
    return y

@@ -1,0 +1,286 @@
+from contextlib import ExitStack
+
+import concourse.mybir as mybir
+from concourse.masks import make_identity
+
+B, N, T, D, DV, NQ = 2, 1024, 4096, 512, 256, 256
+PAGE = 512
+FLOPS = 2 * B * NQ * N * (D + DV)
+
+F32 = mybir.dt.float32
+BF16 = mybir.dt.bfloat16
+I32 = mybir.dt.int32
+U32 = mybir.dt.uint32
+U16 = mybir.dt.uint16
+U8 = mybir.dt.uint8
+FP8X4 = mybir.dt.float8_e4m3fn_x4
+ALU = mybir.AluOpType
+ACT = mybir.ActivationFunctionType
+
+P = 128
+PACK = 4
+PAGES = N // PAGE
+TILES = B * NQ // P
+HALVES = NQ // P
+ROW = N + PACK
+PLANE = 264
+VS_ROW = 8
+V_PLANE = 4
+
+
+def tile_attend_pkv8_sink_kernel(tc, qT, k_words, k_scales, v_words, v_scales, vs, sink, offs, voffs, out):
+    nc = tc.nc
+    with ExitStack() as ctx:
+        keep = ctx.enter_context(tc.tile_pool(name="keep", bufs=1))
+        psum = ctx.enter_context(tc.psum_pool(name="psum", bufs=1))
+
+        offsets = keep.tile([P, B * N // 16], U16, name="offsets")
+        voffsets = keep.tile([P, B * PAGES * DV // 16], U16, name="voffsets")
+        nc.sync.dma_start(offsets[:], offs)
+        nc.sync.dma_start(voffsets[:], voffs)
+
+        ks_pool = keep.tile([P, T // 4], I32, name="ks_pool", tag="reused", align_bytes=64)
+        vs_pool = keep.tile([P, T], F32, name="vs_pool")
+        vsc_pool = keep.tile([P, T // PAGE * DV // 4], I32, name="vsc_pool")
+        nc.vector.memset(ks_pool[:], 0)
+        nc.vector.memset(vs_pool[:], 0.0)
+        nc.vector.memset(vsc_pool[:], 0)
+
+        ident = keep.tile([P, P], F32, name="ident")
+        make_identity(nc, ident[:])
+        neg = keep.tile([P, TILES, ROW], F32, name="neg")
+        eighty = keep.tile([P, TILES, PACK - 1], F32, name="eighty")
+        nc.gpsimd.memset(eighty[:], 80.0)
+        nc.scalar.activation(out=neg[:, :, N + 1 : ROW], in_=eighty[:], func=ACT.Exp)
+
+        for r in range(4):
+            nc.sync.dma_start(ks_pool[r:P:32, :], k_scales[0, r:16:4, :].bitcast(I32))
+        q_raw = [keep.tile([P, PACK, NQ], F32, name="q_raw%d" % b) for b in range(B)]
+        kw_pool = keep.tile([P, T], I32, name="kw_pool")
+        nc.sync.dma_start(q_raw[0][:], qT[0].rearrange("(p j) q -> p j q", j=PACK))
+        nc.sync.dma_start(kw_pool[:], k_words[0].rearrange("p t r -> p (t r)").bitcast(I32))
+        nc.sync.dma_start(q_raw[1][:], qT[1].rearrange("(p j) q -> p j q", j=PACK))
+
+        nc.scalar.dma_start(vs_pool[VS_ROW : VS_ROW + 1, :], vs[0:1, :])
+        for r in range(4):
+            nc.scalar.dma_start(
+                vsc_pool[V_PLANE + r : P : 32, :].rearrange("f (u e) -> f u e", u=T // PAGE),
+                v_scales[:, r:16:4, :].rearrange("u f e -> f u e").bitcast(I32),
+            )
+        sinks = keep.tile([P, TILES], F32, name="sinks")
+        with nc.allow_non_contiguous_dma(reason="one sink a query row"):
+            nc.scalar.dma_start(sinks[:], sink.rearrange("b (h p) o -> p (b h o)", p=P))
+
+        ks = keep.tile([P, B * N], U8, name="ks", align_bytes=64)
+        nc.vector.tensor_copy(ks[:], ks_pool[:].bitcast(U8).indirect(offsets[:]))
+        vw_pool = keep.tile([P, T // PAGE * DV], I32, name="vw_pool", tag="reused", align_bytes=64)
+        nc.sync.dma_start(
+            vw_pool[:].rearrange("p (u e) -> p u e", e=DV),
+            v_words.rearrange("u p e r -> p u (e r)").bitcast(I32),
+        )
+        vs_slots = keep.tile([P, B * N], F32, name="vs_slots")
+        nc.vector.tensor_copy(vs_slots[:], vs_pool[:].indirect(offsets[:]))
+        vsc = keep.tile([P, B * PAGES * DV], U8, name="vsc", align_bytes=64)
+        nc.vector.tensor_copy(vsc[:], vsc_pool[:].bitcast(U8).indirect(voffsets[:]))
+
+        q_bf = [keep.tile([P, NQ, PACK], BF16, name="q_bf%d" % b, align_bytes=64) for b in range(B)]
+        q_codes = [keep.tile([P, NQ], U32, name="q_codes%d" % b, align_bytes=64) for b in range(B)]
+        q_scales = [keep.tile([P, NQ], U8, name="q_scales%d" % b, align_bytes=64) for b in range(B)]
+
+        def cast_q(b):
+            nc.scalar.copy(
+                out=q_bf[b][:].rearrange("p (c i) j -> p c j i", i=4),
+                in_=q_raw[b][:].rearrange("p j (c i) -> p c j i", i=4),
+            )
+
+        def quantize_q(b):
+            nc.vector.quantize_mx(
+                out=q_codes[b][:].bitcast(FP8X4),
+                scales=q_scales[b][:],
+                in_=q_bf[b][:].rearrange("p q j -> p (q j)"),
+            )
+
+        cast_q(0)
+        quantize_q(0)
+
+        vs_cols = keep.tile([P, B * PAGES, PACK], F32, name="vs_cols")
+        for g in range(B * PAGES):
+            bank = psum.tile([P, PACK, P], F32, name="turned", tag="turned", bufs=3)
+            for t in range(PACK):
+                nc.tensor.transpose(bank[:, t, :], vs_slots[:, g * PAGE + t : (g + 1) * PAGE : PACK], ident[:])
+            nc.scalar.copy(out=vs_cols[:, g, :], in_=bank[:, :, VS_ROW])
+        nc.vector.tensor_scalar(
+            out=neg[:, :, N], in0=sinks[:], scalar1=-1.0, scalar2=None, op0=ALU.mult
+        )
+
+        kw = keep.tile([P, B * N], U32, name="kw", align_bytes=64)
+        vw = keep.tile([P, B * PAGES * DV], U32, name="vw", align_bytes=64)
+        neg_max = keep.tile([P, TILES, PAGES], F32, name="neg_max")
+        total = keep.tile([P, TILES], F32, name="total")
+        inverse = keep.tile([P, TILES], F32, name="inverse")
+        prob = [keep.tile([P, PACK, PLANE], F32, name="prob%d" % c) for c in range(TILES)]
+        w_bf = [keep.tile([P, PAGES, P, PACK], BF16, name="w_bf%d" % c, align_bytes=64) for c in range(TILES)]
+        w_codes = [keep.tile([P, PAGES, P], U32, name="w_codes%d" % c, align_bytes=64) for c in range(TILES)]
+        w_scales = [keep.tile([P, PAGES, P], U8, name="w_scales%d" % c, align_bytes=64) for c in range(TILES)]
+        scores = {}
+        turned = {}
+        sums = {}
+
+        def gather_keys(g):
+            nc.vector.tensor_copy(
+                kw[:, g * PAGE : (g + 1) * PAGE],
+                kw_pool[:].bitcast(U32).indirect(offsets[:, g * PAGE // 16 : (g + 1) * PAGE // 16]),
+            )
+
+        def gather_values(b):
+            width = PAGES * DV
+            nc.vector.tensor_copy(
+                vw[:, b * width : (b + 1) * width],
+                vw_pool[:].bitcast(U32).indirect(voffsets[:, b * width // 16 : (b + 1) * width // 16]),
+            )
+
+        def score(c, e):
+            b, h = divmod(c, HALVES)
+            g = b * PAGES + e
+            bank = psum.tile([P, PAGE], F32, name="scores", tag="scores", bufs=3)
+            nc.tensor.matmul_mx(
+                out=bank[:],
+                lhsT=q_codes[b][:, h * P : (h + 1) * P].bitcast(FP8X4),
+                lhsT_scale=q_scales[b][:, h * P : (h + 1) * P],
+                rhs=kw[:, g * PAGE : (g + 1) * PAGE].bitcast(FP8X4),
+                rhs_scale=ks[:, g * PAGE : (g + 1) * PAGE],
+                start=True,
+                stop=True,
+            )
+            scores[c, e] = bank
+
+        def row_max(c, e):
+            first = neg[:, c, N : N + 1] if e == 0 else neg_max[:, c, e - 1 : e]
+            nc.vector.tensor_scalar(
+                out=neg[:, c, e * PAGE : (e + 1) * PAGE],
+                in0=scores[c, e][:],
+                scalar1=-1.0,
+                scalar2=first,
+                op0=ALU.mult,
+                op1=ALU.min,
+                accum_out=neg_max[:, c, e : e + 1],
+            )
+
+        def exponentiate(c):
+            nc.scalar.activation(
+                out=prob[c][:, :, 0 : ROW // PACK].rearrange("p t s -> p s t"),
+                in_=neg[:, c, :].rearrange("p (s t) -> p s t", t=PACK),
+                func=ACT.Exp,
+                scale=-1.0,
+                bias=neg_max[:, c, PAGES - 1 : PAGES],
+                accum_out=total[:, c : c + 1],
+            )
+
+        def turn(c, e):
+            bank = psum.tile([P, PACK, P], F32, name="turned", tag="turned", bufs=3)
+            for t in range(PACK):
+                nc.tensor.transpose(bank[:, t, :], prob[c][:, t, e * P : (e + 1) * P], ident[:])
+            turned[c, e] = bank
+
+        def weigh(c, e):
+            g = c // HALVES * PAGES + e
+            nc.vector.tensor_tensor(
+                out=w_bf[c][:, e, :, :],
+                in0=turned[c, e][:].rearrange("p t q -> p q t"),
+                in1=vs_cols[:, g, :].unsqueeze(1).to_broadcast([P, P, PACK]),
+                op=ALU.mult,
+            )
+
+        def quantize_w(c, e0, e1):
+            nc.vector.quantize_mx(
+                out=w_codes[c][:, e0:e1, :].rearrange("p e q -> p (e q)").bitcast(FP8X4),
+                scales=w_scales[c][:, e0:e1, :].rearrange("p e q -> p (e q)"),
+                in_=w_bf[c][:, e0:e1, :, :].rearrange("p e q t -> p (e q t)"),
+            )
+
+        def multiply(c, e):
+            g = c // HALVES * PAGES + e
+            if e == 0:
+                sums[c] = psum.tile([P, DV], F32, name="sums", tag="sums", bufs=2)
+            nc.tensor.matmul_mx(
+                out=sums[c][:],
+                lhsT=w_codes[c][:, e, :].bitcast(FP8X4),
+                lhsT_scale=w_scales[c][:, e, :],
+                rhs=vw[:, g * DV : (g + 1) * DV].bitcast(FP8X4),
+                rhs_scale=vsc[V_PLANE:P, g * DV : (g + 1) * DV],
+                start=(e == 0),
+                stop=(e == PAGES - 1),
+            )
+
+        def invert(c0, c1):
+            nc.vector.reciprocal(out=inverse[:, c0:c1], in_=total[:, c0:c1])
+
+        def finish(c):
+            b, h = divmod(c, HALVES)
+            y = keep.tile([P, DV], F32, name="y%d" % c)
+            nc.scalar.activation(out=y[:], in_=sums[c][:], func=ACT.Copy, scale=inverse[:, c : c + 1])
+            nc.sync.dma_start(out[b, h * P : (h + 1) * P, :], y[:])
+
+        gather_keys(0)
+        score(0, 0)
+        gather_keys(1)
+        score(0, 1)
+        score(1, 0)
+        gather_keys(2)
+        cast_q(1)
+        row_max(0, 0)
+        score(1, 1)
+        gather_keys(3)
+        row_max(0, 1)
+        exponentiate(0)
+        row_max(1, 0)
+        quantize_q(1)
+        score(2, 0)
+        score(2, 1)
+        row_max(1, 1)
+        score(3, 0)
+        exponentiate(1)
+        row_max(2, 0)
+        score(3, 1)
+        turn(0, 0)
+        turn(0, 1)
+        gather_values(0)
+        row_max(2, 1)
+        exponentiate(2)
+        row_max(3, 0)
+        weigh(0, 0)
+        turn(1, 0)
+        row_max(3, 1)
+        exponentiate(3)
+        weigh(0, 1)
+        turn(1, 1)
+        weigh(1, 0)
+        turn(2, 0)
+        quantize_w(0, 0, 2)
+        invert(0, 2)
+        multiply(0, 0)
+        multiply(0, 1)
+        finish(0)
+        weigh(1, 1)
+        turn(2, 1)
+        gather_values(1)
+        quantize_w(1, 0, 2)
+        multiply(1, 0)
+        multiply(1, 1)
+        finish(1)
+        weigh(2, 0)
+        turn(3, 0)
+        weigh(2, 1)
+        turn(3, 1)
+        weigh(3, 0)
+        quantize_w(2, 0, 2)
+        invert(2, 4)
+        multiply(2, 0)
+        multiply(2, 1)
+        finish(2)
+        weigh(3, 1)
+        quantize_w(3, 0, 1)
+        multiply(3, 0)
+        quantize_w(3, 1, 2)
+        multiply(3, 1)
+        finish(3)

@@ -26,22 +26,23 @@ ROW = N + PACK
 PLANE = 264
 VS_ROW = 8
 V_PLANE = 4
+TURNED_BANK = (1, 2, 3, 0, 4, 5, 6, 7)
 
 
 def tile_attend_pkv8_sink_kernel(tc, qT, k_words, k_scales, v_words, v_scales, vs, sink, offs, voffs, out):
     nc = tc.nc
     with ExitStack() as ctx:
         keep = ctx.enter_context(tc.tile_pool(name="keep", bufs=1))
+        turns = ctx.enter_context(tc.tile_pool(name="turns", bufs=1))
         psum = ctx.enter_context(tc.psum_pool(name="psum", bufs=1))
 
         offsets = keep.tile([P, B * N // 16], U16, name="offsets")
         voffsets = keep.tile([P, B * PAGES * DV // 16], U16, name="voffsets")
         nc.sync.dma_start(offsets[:], offs)
-        nc.sync.dma_start(voffsets[:], voffs)
 
-        ks_pool = keep.tile([P, T // 4], I32, name="ks_pool", tag="reused", align_bytes=64)
-        vs_pool = keep.tile([P, T], F32, name="vs_pool")
-        vsc_pool = keep.tile([P, T // PAGE * DV // 4], I32, name="vsc_pool")
+        ks_pool = turns.tile([P, T // 4], I32, name="ks_pool", offset=18432)
+        vs_pool = turns.tile([P, T], F32, name="vs_pool", offset=2048)
+        vsc_pool = turns.tile([P, T // PAGE * DV // 4], I32, name="vsc_pool", offset=0)
         nc.vector.memset(ks_pool[:], 0)
         nc.vector.memset(vs_pool[:], 0.0)
         nc.vector.memset(vsc_pool[:], 0)
@@ -55,8 +56,9 @@ def tile_attend_pkv8_sink_kernel(tc, qT, k_words, k_scales, v_words, v_scales, v
 
         for r in range(4):
             nc.sync.dma_start(ks_pool[r:P:32, :], k_scales[0, r:16:4, :].bitcast(I32))
+        nc.sync.dma_start(voffsets[:], voffs)
         q_raw = [keep.tile([P, PACK, NQ], F32, name="q_raw%d" % b) for b in range(B)]
-        kw_pool = keep.tile([P, T], I32, name="kw_pool")
+        kw_pool = turns.tile([P, T], I32, name="kw_pool", offset=24576)
         nc.sync.dma_start(q_raw[0][:], qT[0].rearrange("(p j) q -> p j q", j=PACK))
         nc.sync.dma_start(kw_pool[:], k_words[0].rearrange("p t r -> p (t r)").bitcast(I32))
         nc.sync.dma_start(q_raw[1][:], qT[1].rearrange("(p j) q -> p j q", j=PACK))
@@ -67,24 +69,28 @@ def tile_attend_pkv8_sink_kernel(tc, qT, k_words, k_scales, v_words, v_scales, v
                 vsc_pool[V_PLANE + r : P : 32, :].rearrange("f (u e) -> f u e", u=T // PAGE),
                 v_scales[:, r:16:4, :].rearrange("u f e -> f u e").bitcast(I32),
             )
-        sinks = keep.tile([P, TILES], F32, name="sinks")
-        with nc.allow_non_contiguous_dma(reason="one sink a query row"):
-            nc.scalar.dma_start(sinks[:], sink.rearrange("b (h p) o -> p (b h o)", p=P))
 
         ks = keep.tile([P, B * N], U8, name="ks", align_bytes=64)
         nc.vector.tensor_copy(ks[:], ks_pool[:].bitcast(U8).indirect(offsets[:]))
-        vw_pool = keep.tile([P, T // PAGE * DV], I32, name="vw_pool", tag="reused", align_bytes=64)
+        sink_rows = turns.tile([P, P], F32, name="sink_rows", offset=20480)
+        nc.gpsimd.memset(sink_rows[:], 0.0)
+        nc.scalar.dma_start(sink_rows[0:TILES, :], sink.rearrange("b (h p) o -> (b h) (p o)", p=P))
+        vs_slots = keep.tile([P, B * N], F32, name="vs_slots")
+        for b in range(B):
+            nc.vector.tensor_copy(
+                vs_slots[:, b * N : (b + 1) * N],
+                vs_pool[:].indirect(offsets[:, b * N // 16 : (b + 1) * N // 16]),
+            )
+        vw_pool = turns.tile([P, T // PAGE * DV], I32, name="vw_pool", offset=12288)
         nc.sync.dma_start(
             vw_pool[:].rearrange("p (u e) -> p u e", e=DV),
             v_words.rearrange("u p e r -> p u (e r)").bitcast(I32),
         )
-        vs_slots = keep.tile([P, B * N], F32, name="vs_slots")
-        nc.vector.tensor_copy(vs_slots[:], vs_pool[:].indirect(offsets[:]))
-        vsc = keep.tile([P, B * PAGES * DV], U8, name="vsc", align_bytes=64)
+        vsc = turns.tile([P, B * PAGES * DV], U8, name="vsc", align_bytes=64, offset=8192)
         nc.vector.tensor_copy(vsc[:], vsc_pool[:].bitcast(U8).indirect(voffsets[:]))
 
-        q_bf = [keep.tile([P, NQ, PACK], BF16, name="q_bf%d" % b, align_bytes=64) for b in range(B)]
-        q_codes = [keep.tile([P, NQ], U32, name="q_codes%d" % b, align_bytes=64) for b in range(B)]
+        q_bf = [turns.tile([P, NQ, PACK], BF16, name="q_bf%d" % b, align_bytes=64, offset=40960 + 2048 * b) for b in range(B)]
+        q_codes = [turns.tile([P, NQ], U32, name="q_codes0", align_bytes=64, offset=9216)]
         q_scales = [keep.tile([P, NQ], U8, name="q_scales%d" % b, align_bytes=64) for b in range(B)]
 
         def cast_q(b):
@@ -104,17 +110,20 @@ def tile_attend_pkv8_sink_kernel(tc, qT, k_words, k_scales, v_words, v_scales, v
         quantize_q(0)
 
         vs_cols = keep.tile([P, B * PAGES, PACK], F32, name="vs_cols")
-        for g in range(B * PAGES):
-            bank = psum.tile([P, PACK, P], F32, name="turned", tag="turned", bufs=3)
+
+        def turn_vs(g, index):
+            bank = psum.tile([P, PACK, P], F32, name="vs_turned", tag="bank%d" % index)
             for t in range(PACK):
                 nc.tensor.transpose(bank[:, t, :], vs_slots[:, g * PAGE + t : (g + 1) * PAGE : PACK], ident[:])
             nc.scalar.copy(out=vs_cols[:, g, :], in_=bank[:, :, VS_ROW])
-        nc.vector.tensor_scalar(
-            out=neg[:, :, N], in0=sinks[:], scalar1=-1.0, scalar2=None, op0=ALU.mult
-        )
 
-        kw = keep.tile([P, B * N], U32, name="kw", align_bytes=64)
-        vw = keep.tile([P, B * PAGES * DV], U32, name="vw", align_bytes=64)
+        for g in range(B * PAGES - 1):
+            turn_vs(g, 4 + g)
+        sink_bank = psum.tile([P, P], F32, name="sink_bank", tag="bank7")
+        nc.tensor.transpose(sink_bank[:], sink_rows[:], ident[:])
+        nc.scalar.activation(out=neg[:, :, N], in_=sink_bank[:, 0:TILES], func=ACT.Copy, scale=-1.0)
+
+        kw = turns.tile([P, B * N], U32, name="kw", align_bytes=64, offset=0)
         neg_max = keep.tile([P, TILES, PAGES], F32, name="neg_max")
         total = keep.tile([P, TILES], F32, name="total")
         inverse = keep.tile([P, TILES], F32, name="inverse")
@@ -142,7 +151,7 @@ def tile_attend_pkv8_sink_kernel(tc, qT, k_words, k_scales, v_words, v_scales, v
         def score(c, e):
             b, h = divmod(c, HALVES)
             g = b * PAGES + e
-            bank = psum.tile([P, PAGE], F32, name="scores", tag="scores", bufs=3)
+            bank = psum.tile([P, PAGE], F32, name="scores", tag="bank%d" % (c * PAGES + e))
             nc.tensor.matmul_mx(
                 out=bank[:],
                 lhsT=q_codes[b][:, h * P : (h + 1) * P].bitcast(FP8X4),
@@ -177,7 +186,7 @@ def tile_attend_pkv8_sink_kernel(tc, qT, k_words, k_scales, v_words, v_scales, v
             )
 
         def turn(c, e):
-            bank = psum.tile([P, PACK, P], F32, name="turned", tag="turned", bufs=3)
+            bank = psum.tile([P, PACK, P], F32, name="turned", tag="bank%d" % TURNED_BANK[c * PAGES + e])
             for t in range(PACK):
                 nc.tensor.transpose(bank[:, t, :], prob[c][:, t, e * P : (e + 1) * P], ident[:])
             turned[c, e] = bank
@@ -201,7 +210,7 @@ def tile_attend_pkv8_sink_kernel(tc, qT, k_words, k_scales, v_words, v_scales, v
         def multiply(c, e):
             g = c // HALVES * PAGES + e
             if e == 0:
-                sums[c] = psum.tile([P, DV], F32, name="sums", tag="sums", bufs=2)
+                sums[c] = psum.tile([P, DV], F32, name="sums", tag="bank%d" % ((c + 1) % TILES))
             nc.tensor.matmul_mx(
                 out=sums[c][:],
                 lhsT=w_codes[c][:, e, :].bitcast(FP8X4),
@@ -228,13 +237,16 @@ def tile_attend_pkv8_sink_kernel(tc, qT, k_words, k_scales, v_words, v_scales, v
         score(1, 0)
         gather_keys(2)
         cast_q(1)
-        row_max(0, 0)
         score(1, 1)
+        row_max(0, 0)
+        turn_vs(B * PAGES - 1, 0)
         gather_keys(3)
         row_max(0, 1)
         exponentiate(0)
         row_max(1, 0)
+        q_codes.append(turns.tile([P, NQ], U32, name="q_codes1", align_bytes=64, offset=24576))
         quantize_q(1)
+        vw = turns.tile([P, B * PAGES * DV], U32, name="vw", align_bytes=64, offset=43008)
         score(2, 0)
         score(2, 1)
         row_max(1, 1)

@@ -49,7 +49,7 @@ def tile_attend_pkv8_sink_kernel(tc, qT, k_words, k_scales, v_words, v_scales, v
 
         ident = keep.tile([P, P], F32, name="ident")
         make_identity(nc, ident[:])
-        neg = keep.tile([P, TILES, ROW], F32, name="neg")
+        neg = turns.tile([P, TILES, ROW], F32, name="neg", offset=49152)
         eighty = keep.tile([P, TILES, PACK - 1], F32, name="eighty")
         nc.gpsimd.memset(eighty[:], 80.0)
         nc.scalar.activation(out=neg[:, :, N + 1 : ROW], in_=eighty[:], func=ACT.Exp)
@@ -128,7 +128,7 @@ def tile_attend_pkv8_sink_kernel(tc, qT, k_words, k_scales, v_words, v_scales, v
         total = keep.tile([P, TILES], F32, name="total")
         inverse = keep.tile([P, TILES], F32, name="inverse")
         prob = [keep.tile([P, PACK, PLANE], F32, name="prob%d" % c) for c in range(TILES)]
-        w_bf = [keep.tile([P, PAGES, P, PACK], BF16, name="w_bf%d" % c, align_bytes=64) for c in range(TILES)]
+        w_bf = {c: keep.tile([P, PAGES, P, PACK], BF16, name="w_bf%d" % c, align_bytes=64) for c in (0, 1, 3)}
         w_codes = [keep.tile([P, PAGES, P], U32, name="w_codes%d" % c, align_bytes=64) for c in range(TILES)]
         w_scales = [keep.tile([P, PAGES, P], U8, name="w_scales%d" % c, align_bytes=64) for c in range(TILES)]
         scores = {}
@@ -200,6 +200,16 @@ def tile_attend_pkv8_sink_kernel(tc, qT, k_words, k_scales, v_words, v_scales, v
                 op=ALU.mult,
             )
 
+        def weigh_on_scalar(c, e):
+            g = c // HALVES * PAGES + e
+            for t in range(PACK):
+                nc.scalar.activation(
+                    out=w_bf[c][:, e, :, t],
+                    in_=turned[c, e][:, t, :],
+                    func=ACT.Copy,
+                    scale=vs_cols[:, g, t : t + 1],
+                )
+
         def quantize_w(c, e0, e1):
             nc.vector.quantize_mx(
                 out=w_codes[c][:, e0:e1, :].rearrange("p e q -> p (e q)").bitcast(FP8X4),
@@ -227,7 +237,12 @@ def tile_attend_pkv8_sink_kernel(tc, qT, k_words, k_scales, v_words, v_scales, v
         def finish(c):
             b, h = divmod(c, HALVES)
             y = keep.tile([P, DV], F32, name="y%d" % c)
-            nc.scalar.activation(out=y[:], in_=sums[c][:], func=ACT.Copy, scale=inverse[:, c : c + 1])
+            if c < HALVES:
+                nc.scalar.activation(out=y[:], in_=sums[c][:], func=ACT.Copy, scale=inverse[:, c : c + 1])
+            else:
+                nc.vector.tensor_scalar(
+                    out=y[:], in0=sums[c][:], scalar1=inverse[:, c : c + 1], scalar2=None, op0=ALU.mult
+                )
             nc.sync.dma_start(out[b, h * P : (h + 1) * P, :], y[:])
 
         gather_keys(0)
@@ -243,56 +258,57 @@ def tile_attend_pkv8_sink_kernel(tc, qT, k_words, k_scales, v_words, v_scales, v
         gather_keys(3)
         row_max(0, 1)
         exponentiate(0)
-        row_max(1, 0)
         q_codes.append(turns.tile([P, NQ], U32, name="q_codes1", align_bytes=64, offset=24576))
         quantize_q(1)
         vw = turns.tile([P, B * PAGES * DV], U32, name="vw", align_bytes=64, offset=43008)
         score(2, 0)
-        score(2, 1)
-        row_max(1, 1)
         score(3, 0)
+        score(2, 1)
+        score(3, 1)
+        row_max(1, 0)
+        gather_values(0)
+        row_max(1, 1)
         exponentiate(1)
         row_max(2, 0)
-        score(3, 1)
         turn(0, 0)
         turn(0, 1)
-        gather_values(0)
+        row_max(3, 0)
         row_max(2, 1)
         exponentiate(2)
-        row_max(3, 0)
-        weigh(0, 0)
         turn(1, 0)
         row_max(3, 1)
         exponentiate(3)
-        weigh(0, 1)
+        weigh(0, 0)
         turn(1, 1)
-        weigh(1, 0)
         turn(2, 0)
+        turn(2, 1)
+        w_bf[2] = turns.tile([P, PAGES, P, PACK], BF16, name="w_bf2", align_bytes=64, offset=49152)
+        weigh_on_scalar(2, 0)
+        weigh_on_scalar(2, 1)
+        weigh(0, 1)
+        weigh(1, 0)
+        turn(3, 0)
+        turn(3, 1)
         quantize_w(0, 0, 2)
-        invert(0, 2)
         multiply(0, 0)
         multiply(0, 1)
-        finish(0)
         weigh(1, 1)
-        turn(2, 1)
         gather_values(1)
         quantize_w(1, 0, 2)
         multiply(1, 0)
         multiply(1, 1)
+        invert(0, 4)
+        finish(0)
         finish(1)
-        weigh(2, 0)
-        turn(3, 0)
-        weigh(2, 1)
-        turn(3, 1)
         weigh(3, 0)
-        quantize_w(2, 0, 2)
-        invert(2, 4)
+        quantize_w(2, 0, 1)
         multiply(2, 0)
-        multiply(2, 1)
-        finish(2)
         weigh(3, 1)
         quantize_w(3, 0, 1)
         multiply(3, 0)
         quantize_w(3, 1, 2)
         multiply(3, 1)
+        quantize_w(2, 1, 2)
+        multiply(2, 1)
         finish(3)
+        finish(2)

@@ -38,14 +38,17 @@ def tile_attend_pkv8_sink_kernel(tc, qT, k_words, k_scales, v_words, v_scales, v
 
         offsets = keep.tile([P, B * N // 16], U16, name="offsets")
         voffsets = keep.tile([P, B * PAGES * DV // 16], U16, name="voffsets")
+        nc.sync.dma_start(voffsets[:], voffs)
         nc.sync.dma_start(offsets[:], offs)
 
         ks_pool = turns.tile([P, T // 4], I32, name="ks_pool", offset=18432)
         vs_pool = turns.tile([P, T], F32, name="vs_pool", offset=2048)
         vsc_pool = turns.tile([P, T // PAGE * DV // 4], I32, name="vsc_pool", offset=0)
+        nc.vector.memset(vsc_pool[:], 0)
         nc.vector.memset(ks_pool[:], 0)
         nc.vector.memset(vs_pool[:], 0.0)
-        nc.vector.memset(vsc_pool[:], 0)
+        sink_rows = keep.tile([P, P], F32, name="sink_rows")
+        nc.gpsimd.memset(sink_rows[:], 0.0)
 
         ident = keep.tile([P, P], F32, name="ident")
         make_identity(nc, ident[:])
@@ -55,26 +58,25 @@ def tile_attend_pkv8_sink_kernel(tc, qT, k_words, k_scales, v_words, v_scales, v
         nc.scalar.activation(out=neg[:, :, N + 1 : ROW], in_=eighty[:], func=ACT.Exp)
 
         for r in range(4):
-            nc.sync.dma_start(ks_pool[r:P:32, :], k_scales[0, r:16:4, :].bitcast(I32))
-        nc.sync.dma_start(voffsets[:], voffs)
-        q_raw = [keep.tile([P, PACK, NQ], F32, name="q_raw%d" % b) for b in range(B)]
-        kw_pool = turns.tile([P, T], I32, name="kw_pool", offset=24576)
-        nc.sync.dma_start(q_raw[0][:], qT[0].rearrange("(p j) q -> p j q", j=PACK))
-        nc.sync.dma_start(kw_pool[:], k_words[0].rearrange("p t r -> p (t r)").bitcast(I32))
-        nc.sync.dma_start(q_raw[1][:], qT[1].rearrange("(p j) q -> p j q", j=PACK))
-
-        nc.scalar.dma_start(vs_pool[VS_ROW : VS_ROW + 1, :], vs[0:1, :])
-        for r in range(4):
-            nc.scalar.dma_start(
+            nc.sync.dma_start(
                 vsc_pool[V_PLANE + r : P : 32, :].rearrange("f (u e) -> f u e", u=T // PAGE),
                 v_scales[:, r:16:4, :].rearrange("u f e -> f u e").bitcast(I32),
             )
+        for r in range(4):
+            nc.sync.dma_start(ks_pool[r:P:32, :], k_scales[0, r:16:4, :].bitcast(I32))
+        q_raw = [keep.tile([P, PACK, NQ], F32, name="q_raw%d" % b) for b in range(B)]
+        kw_pool = turns.tile([P, T], I32, name="kw_pool", offset=24576)
+        nc.sync.dma_start(q_raw[0][:], qT[0].rearrange("(p j) q -> p j q", j=PACK))
+        nc.sync.dma_start(vs_pool[VS_ROW : VS_ROW + 1, :], vs[0:1, :])
+        nc.sync.dma_start(sink_rows[0:TILES, :], sink.rearrange("b (h p) o -> (b h) (p o)", p=P))
+        nc.sync.dma_start(kw_pool[:], k_words[0].rearrange("p t r -> p (t r)").bitcast(I32))
+        nc.sync.dma_start(q_raw[1][:], qT[1].rearrange("(p j) q -> p j q", j=PACK))
+
+        vsc = keep.tile([P, B * PAGES * DV], U8, name="vsc", align_bytes=64)
+        nc.vector.tensor_copy(vsc[:], vsc_pool[:].bitcast(U8).indirect(voffsets[:]))
 
         ks = keep.tile([P, B * N], U8, name="ks", align_bytes=64)
         nc.vector.tensor_copy(ks[:], ks_pool[:].bitcast(U8).indirect(offsets[:]))
-        sink_rows = turns.tile([P, P], F32, name="sink_rows", offset=20480)
-        nc.gpsimd.memset(sink_rows[:], 0.0)
-        nc.scalar.dma_start(sink_rows[0:TILES, :], sink.rearrange("b (h p) o -> (b h) (p o)", p=P))
         vs_slots = keep.tile([P, B * N], F32, name="vs_slots")
         for b in range(B):
             nc.vector.tensor_copy(
@@ -86,8 +88,6 @@ def tile_attend_pkv8_sink_kernel(tc, qT, k_words, k_scales, v_words, v_scales, v
             vw_pool[:].rearrange("p (u e) -> p u e", e=DV),
             v_words.rearrange("u p e r -> p u (e r)").bitcast(I32),
         )
-        vsc = turns.tile([P, B * PAGES * DV], U8, name="vsc", align_bytes=64, offset=8192)
-        nc.vector.tensor_copy(vsc[:], vsc_pool[:].bitcast(U8).indirect(voffsets[:]))
 
         q_bf = [turns.tile([P, NQ, PACK], BF16, name="q_bf%d" % b, align_bytes=64, offset=40960 + 2048 * b) for b in range(B)]
         q_codes = [turns.tile([P, NQ], U32, name="q_codes0", align_bytes=64, offset=9216)]

@@ -43,15 +43,13 @@ def tile_attend_pkv8_sink_kernel(tc, qT, k_words, k_scales, v_words, v_scales, v
 
         ks_pool = turns.tile([P, T // 4], I32, name="ks_pool", offset=18432)
         vs_pool = turns.tile([P, T], F32, name="vs_pool", offset=2048)
-        vsc_pool = turns.tile([P, T // PAGE * DV // 4], I32, name="vsc_pool", offset=0)
+        vsc_pool = turns.tile([P, T // PAGE * DV // 4], I32, name="vsc_pool", offset=66048)
         nc.vector.memset(vsc_pool[:], 0)
         nc.vector.memset(ks_pool[:], 0)
         nc.vector.memset(vs_pool[:], 0.0)
         sink_rows = keep.tile([P, P], F32, name="sink_rows")
         nc.gpsimd.memset(sink_rows[:], 0.0)
 
-        ident = keep.tile([P, P], F32, name="ident")
-        make_identity(nc, ident[:])
         neg = turns.tile([P, TILES, ROW], F32, name="neg", offset=49152)
         eighty = keep.tile([P, TILES, PACK - 1], F32, name="eighty")
         nc.gpsimd.memset(eighty[:], 80.0)
@@ -74,6 +72,8 @@ def tile_attend_pkv8_sink_kernel(tc, qT, k_words, k_scales, v_words, v_scales, v
 
         vsc = keep.tile([P, B * PAGES * DV], U8, name="vsc", align_bytes=64)
         nc.vector.tensor_copy(vsc[:], vsc_pool[:].bitcast(U8).indirect(voffsets[:]))
+        ident = turns.tile([P, P], F32, name="ident", offset=66048)
+        make_identity(nc, ident[:])
 
         ks = keep.tile([P, B * N], U8, name="ks", align_bytes=64)
         nc.vector.tensor_copy(ks[:], ks_pool[:].bitcast(U8).indirect(offsets[:]))
@@ -256,20 +256,18 @@ def tile_attend_pkv8_sink_kernel(tc, qT, k_words, k_scales, v_words, v_scales, v
         row_max(0, 0)
         turn_vs(B * PAGES - 1, 0)
         gather_keys(3)
-        row_max(0, 1)
-        exponentiate(0)
         q_codes.append(turns.tile([P, NQ], U32, name="q_codes1", align_bytes=64, offset=24576))
         quantize_q(1)
-        vw = turns.tile([P, B * PAGES * DV], U32, name="vw", align_bytes=64, offset=43008)
         score(2, 0)
         score(3, 0)
         score(2, 1)
         score(3, 1)
+        row_max(0, 1)
+        exponentiate(0)
         row_max(1, 0)
-        gather_values(0)
+        row_max(2, 0)
         row_max(1, 1)
         exponentiate(1)
-        row_max(2, 0)
         turn(0, 0)
         turn(0, 1)
         row_max(3, 0)
@@ -278,6 +276,8 @@ def tile_attend_pkv8_sink_kernel(tc, qT, k_words, k_scales, v_words, v_scales, v
         turn(1, 0)
         row_max(3, 1)
         exponentiate(3)
+        vw = turns.tile([P, B * PAGES * DV], U32, name="vw", align_bytes=64, offset=24576)
+        gather_values(0)
         weigh(0, 0)
         turn(1, 1)
         turn(2, 0)

@@ -22,11 +22,22 @@ PACK = 4
 PAGES = N // PAGE
 TILES = B * NQ // P
 HALVES = NQ // P
-ROW = N + PACK
-PLANE = 264
-VS_ROW = 8
+ROW = N + 8
+VS_ROW = P - 1
 V_PLANE = 4
-TURNED_BANK = (1, 2, 3, 0, 4, 5, 6, 7)
+SCORE_BANK = {(0, 0): 0, (1, 0): 1, (0, 1): 2, (1, 1): 3, (2, 0): 4, (3, 0): 5, (2, 1): 6, (3, 1): 7}
+SUM_BANK = (5, 2, 4, 6)
+
+VS_AT = 2048
+KS_AT = 18432
+KW_POOL_AT = 24576
+Q_BF_AT = 40960
+NEG_AT = 49152
+NEG_BYTES = 4160
+VSC_AT = 66048
+PROB_AT = 68096
+IDENT_AT = 10240
+VW_POOL_AT = 10752
 
 
 def tile_attend_pkv8_sink_kernel(tc, qT, k_words, k_scales, v_words, v_scales, vs, sink, offs, voffs, out):
@@ -38,59 +49,57 @@ def tile_attend_pkv8_sink_kernel(tc, qT, k_words, k_scales, v_words, v_scales, v
 
         offsets = keep.tile([P, B * N // 16], U16, name="offsets")
         voffsets = keep.tile([P, B * PAGES * DV // 16], U16, name="voffsets")
-        nc.sync.dma_start(voffsets[:], voffs)
-        nc.sync.dma_start(offsets[:], offs)
-
-        ks_pool = turns.tile([P, T // 4], I32, name="ks_pool", offset=18432)
-        vs_pool = turns.tile([P, T], F32, name="vs_pool", offset=2048)
-        vsc_pool = turns.tile([P, T // PAGE * DV // 4], I32, name="vsc_pool", offset=66048)
-        nc.vector.memset(vsc_pool[:], 0)
-        nc.vector.memset(ks_pool[:], 0)
-        nc.vector.memset(vs_pool[:], 0.0)
+        ks_pool = turns.tile([P, T // 4], I32, name="ks_pool", offset=KS_AT)
+        vs_pool = turns.tile([P, T], F32, name="vs_pool", offset=VS_AT)
         sink_rows = keep.tile([P, P], F32, name="sink_rows")
+        nc.vector.memset(ks_pool[:], 0)
+        nc.vector.memset(vs_pool[0:VS_ROW, :], 0.0)
+        vsc_pool = turns.tile([P, T // PAGE * DV // 4], I32, name="vsc_pool", offset=VSC_AT)
+        nc.vector.memset(vsc_pool[:], 0)
         nc.gpsimd.memset(sink_rows[:], 0.0)
 
-        neg = turns.tile([P, TILES, ROW], F32, name="neg", offset=49152)
-        eighty = keep.tile([P, TILES, PACK - 1], F32, name="eighty")
-        nc.gpsimd.memset(eighty[:], 80.0)
-        nc.scalar.activation(out=neg[:, :, N + 1 : ROW], in_=eighty[:], func=ACT.Exp)
+        nc.sync.dma_start(offsets[:], offs)
+        nc.sync.dma_start(vs_pool[VS_ROW:P, :], vs[0:1, :])
+        nc.sync.dma_start(voffsets[:], voffs)
+        nc.sync.dma_start(sink_rows[0:TILES, :], sink.rearrange("b (h p) o -> (b h) (p o)", p=P))
+        for r in range(4):
+            nc.sync.dma_start(ks_pool[r:P:32, :], k_scales[0, r:16:4, :].bitcast(I32))
+        q_raw = [keep.tile([P, PACK, NQ], F32, name="q_raw%d" % b) for b in range(B)]
+        kw_pool = turns.tile([P, T], I32, name="kw_pool", offset=KW_POOL_AT)
+        nc.sync.dma_start(q_raw[0][:], qT[0].rearrange("(p j) q -> p j q", j=PACK))
+        nc.sync.dma_start(kw_pool[:], k_words[0].rearrange("p t r -> p (t r)").bitcast(I32))
+        nc.sync.dma_start(q_raw[1][:], qT[1].rearrange("(p j) q -> p j q", j=PACK))
 
         for r in range(4):
             nc.sync.dma_start(
                 vsc_pool[V_PLANE + r : P : 32, :].rearrange("f (u e) -> f u e", u=T // PAGE),
                 v_scales[:, r:16:4, :].rearrange("u f e -> f u e").bitcast(I32),
             )
-        for r in range(4):
-            nc.sync.dma_start(ks_pool[r:P:32, :], k_scales[0, r:16:4, :].bitcast(I32))
-        q_raw = [keep.tile([P, PACK, NQ], F32, name="q_raw%d" % b) for b in range(B)]
-        kw_pool = turns.tile([P, T], I32, name="kw_pool", offset=24576)
-        nc.sync.dma_start(q_raw[0][:], qT[0].rearrange("(p j) q -> p j q", j=PACK))
-        nc.sync.dma_start(vs_pool[VS_ROW : VS_ROW + 1, :], vs[0:1, :])
-        nc.sync.dma_start(sink_rows[0:TILES, :], sink.rearrange("b (h p) o -> (b h) (p o)", p=P))
-        nc.sync.dma_start(kw_pool[:], k_words[0].rearrange("p t r -> p (t r)").bitcast(I32))
-        nc.sync.dma_start(q_raw[1][:], qT[1].rearrange("(p j) q -> p j q", j=PACK))
 
-        vsc = keep.tile([P, B * PAGES * DV], U8, name="vsc", align_bytes=64)
-        nc.vector.tensor_copy(vsc[:], vsc_pool[:].bitcast(U8).indirect(voffsets[:]))
-        ident = turns.tile([P, P], F32, name="ident", offset=66048)
+        neg = [turns.tile([P, ROW], F32, name="neg%d" % c, offset=NEG_AT + c * NEG_BYTES) for c in range(TILES)]
+
+        vs_slots = keep.tile([P, B * N], F32, name="vs_slots")
+        nc.vector.tensor_copy(vs_slots[:], vs_pool[:].indirect(offsets[:]))
+        vs_cols = keep.tile([P, B * PAGES, 2 * PACK], F32, name="vs_cols")
+        for g in range(B * PAGES):
+            nc.sync.dma_start(
+                vs_cols[:, g, 0:PACK],
+                vs_slots[VS_ROW:P, g * PAGE : (g + 1) * PAGE].rearrange("o (p t) -> o p t", t=PACK),
+            )
+        ident = turns.tile([P, P], F32, name="ident", offset=IDENT_AT)
         make_identity(nc, ident[:])
 
         ks = keep.tile([P, B * N], U8, name="ks", align_bytes=64)
         nc.vector.tensor_copy(ks[:], ks_pool[:].bitcast(U8).indirect(offsets[:]))
-        vs_slots = keep.tile([P, B * N], F32, name="vs_slots")
-        for b in range(B):
-            nc.vector.tensor_copy(
-                vs_slots[:, b * N : (b + 1) * N],
-                vs_pool[:].indirect(offsets[:, b * N // 16 : (b + 1) * N // 16]),
-            )
-        vw_pool = turns.tile([P, T // PAGE * DV], I32, name="vw_pool", offset=12288)
+
+        vw_pool = turns.tile([P, T // PAGE * DV], I32, name="vw_pool", offset=VW_POOL_AT)
         nc.sync.dma_start(
             vw_pool[:].rearrange("p (u e) -> p u e", e=DV),
             v_words.rearrange("u p e r -> p u (e r)").bitcast(I32),
         )
 
-        q_bf = [turns.tile([P, NQ, PACK], BF16, name="q_bf%d" % b, align_bytes=64, offset=40960 + 2048 * b) for b in range(B)]
-        q_codes = [turns.tile([P, NQ], U32, name="q_codes0", align_bytes=64, offset=9216)]
+        q_bf = [turns.tile([P, NQ, PACK], BF16, name="q_bf%d" % b, align_bytes=64, offset=Q_BF_AT + 2048 * b) for b in range(B)]
+        q_codes = {}
         q_scales = [keep.tile([P, NQ], U8, name="q_scales%d" % b, align_bytes=64) for b in range(B)]
 
         def cast_q(b):
@@ -100,6 +109,7 @@ def tile_attend_pkv8_sink_kernel(tc, qT, k_words, k_scales, v_words, v_scales, v
             )
 
         def quantize_q(b):
+            q_codes[b] = turns.tile([P, NQ], U32, name="q_codes%d" % b, align_bytes=64, offset=9216)
             nc.vector.quantize_mx(
                 out=q_codes[b][:].bitcast(FP8X4),
                 scales=q_scales[b][:],
@@ -109,54 +119,40 @@ def tile_attend_pkv8_sink_kernel(tc, qT, k_words, k_scales, v_words, v_scales, v
         cast_q(0)
         quantize_q(0)
 
-        vs_cols = keep.tile([P, B * PAGES, PACK], F32, name="vs_cols")
-
-        def turn_vs(g, index):
-            bank = psum.tile([P, PACK, P], F32, name="vs_turned", tag="bank%d" % index)
-            for t in range(PACK):
-                nc.tensor.transpose(bank[:, t, :], vs_slots[:, g * PAGE + t : (g + 1) * PAGE : PACK], ident[:])
-            nc.scalar.copy(out=vs_cols[:, g, :], in_=bank[:, :, VS_ROW])
-
-        for g in range(B * PAGES - 1):
-            turn_vs(g, 4 + g)
         sink_bank = psum.tile([P, P], F32, name="sink_bank", tag="bank7")
         nc.tensor.transpose(sink_bank[:], sink_rows[:], ident[:])
-        nc.scalar.activation(out=neg[:, :, N], in_=sink_bank[:, 0:TILES], func=ACT.Copy, scale=-1.0)
+        for c in range(TILES):
+            nc.scalar.activation(out=neg[c][:, N : N + 1], in_=sink_bank[:, c : c + 1], func=ACT.Copy, scale=-1.0)
+        cast_q(1)
 
-        kw = turns.tile([P, B * N], U32, name="kw", align_bytes=64, offset=0)
-        neg_max = keep.tile([P, TILES, PAGES], F32, name="neg_max")
+        kw = {}
+        KW_AT = (VS_AT, VS_AT + 2048, VS_AT + 2048, NEG_AT)
+        neg_max = {0: keep.tile([P, HALVES, PAGES], F32, name="neg_max0")}
         total = keep.tile([P, TILES], F32, name="total")
-        inverse = keep.tile([P, TILES], F32, name="inverse")
-        prob = [keep.tile([P, PACK, PLANE], F32, name="prob%d" % c) for c in range(TILES)]
-        w_bf = {c: keep.tile([P, PAGES, P, PACK], BF16, name="w_bf%d" % c, align_bytes=64) for c in (0, 1, 3)}
-        w_codes = [keep.tile([P, PAGES, P], U32, name="w_codes%d" % c, align_bytes=64) for c in range(TILES)]
+        prob = {}
+        w_bf = {c: keep.tile([P, PAGES, P, PACK], BF16, name="w_bf%d" % c, align_bytes=64) for c in range(HALVES)}
+        w_codes = {c: keep.tile([P, PAGES, P], U32, name="w_codes%d" % c, align_bytes=64) for c in range(HALVES, TILES)}
         w_scales = [keep.tile([P, PAGES, P], U8, name="w_scales%d" % c, align_bytes=64) for c in range(TILES)]
         scores = {}
         turned = {}
         sums = {}
 
         def gather_keys(g):
+            kw[g] = turns.tile([P, PAGE], U32, name="kw%d" % g, align_bytes=64, offset=KW_AT[g])
             nc.vector.tensor_copy(
-                kw[:, g * PAGE : (g + 1) * PAGE],
+                kw[g][:],
                 kw_pool[:].bitcast(U32).indirect(offsets[:, g * PAGE // 16 : (g + 1) * PAGE // 16]),
-            )
-
-        def gather_values(b):
-            width = PAGES * DV
-            nc.vector.tensor_copy(
-                vw[:, b * width : (b + 1) * width],
-                vw_pool[:].bitcast(U32).indirect(voffsets[:, b * width // 16 : (b + 1) * width // 16]),
             )
 
         def score(c, e):
             b, h = divmod(c, HALVES)
             g = b * PAGES + e
-            bank = psum.tile([P, PAGE], F32, name="scores", tag="bank%d" % (c * PAGES + e))
+            bank = psum.tile([P, PAGE], F32, name="scores", tag="bank%d" % SCORE_BANK[c, e])
             nc.tensor.matmul_mx(
                 out=bank[:],
                 lhsT=q_codes[b][:, h * P : (h + 1) * P].bitcast(FP8X4),
                 lhsT_scale=q_scales[b][:, h * P : (h + 1) * P],
-                rhs=kw[:, g * PAGE : (g + 1) * PAGE].bitcast(FP8X4),
+                rhs=kw[g][:].bitcast(FP8X4),
                 rhs_scale=ks[:, g * PAGE : (g + 1) * PAGE],
                 start=True,
                 stop=True,
@@ -164,31 +160,33 @@ def tile_attend_pkv8_sink_kernel(tc, qT, k_words, k_scales, v_words, v_scales, v
             scores[c, e] = bank
 
         def row_max(c, e):
-            first = neg[:, c, N : N + 1] if e == 0 else neg_max[:, c, e - 1 : e]
+            first = neg[c][:, N : N + 1] if e == 0 else neg_max[c // HALVES][:, c % HALVES, e - 1 : e]
             nc.vector.tensor_scalar(
-                out=neg[:, c, e * PAGE : (e + 1) * PAGE],
-                in0=scores[c, e][:],
+                out=neg[c][:, e * PAGE : (e + 1) * PAGE].rearrange("p (t s) -> p t s", t=PACK),
+                in0=scores[c, e][:].rearrange("p (s t) -> p t s", t=PACK),
                 scalar1=-1.0,
                 scalar2=first,
                 op0=ALU.mult,
                 op1=ALU.min,
-                accum_out=neg_max[:, c, e : e + 1],
+                accum_out=neg_max[c // HALVES][:, c % HALVES, e : e + 1],
             )
 
         def exponentiate(c):
+            prob[c] = turns.tile([P, ROW], F32, name="prob%d" % c, offset=PROB_AT + c * NEG_BYTES)
             nc.scalar.activation(
-                out=prob[c][:, :, 0 : ROW // PACK].rearrange("p t s -> p s t"),
-                in_=neg[:, c, :].rearrange("p (s t) -> p s t", t=PACK),
+                out=prob[c][:, 0 : N + 1],
+                in_=neg[c][:, 0 : N + 1],
                 func=ACT.Exp,
                 scale=-1.0,
-                bias=neg_max[:, c, PAGES - 1 : PAGES],
+                bias=neg_max[c // HALVES][:, c % HALVES, PAGES - 1 : PAGES],
                 accum_out=total[:, c : c + 1],
             )
 
         def turn(c, e):
-            bank = psum.tile([P, PACK, P], F32, name="turned", tag="bank%d" % TURNED_BANK[c * PAGES + e])
+            bank = psum.tile([P, PACK, P], F32, name="turned", tag="bank%d" % (c * PAGES + e))
             for t in range(PACK):
-                nc.tensor.transpose(bank[:, t, :], prob[c][:, t, e * P : (e + 1) * P], ident[:])
+                first = e * PAGE + t * P
+                nc.tensor.transpose(bank[:, t, :], prob[c][:, first : first + P], ident[:])
             turned[c, e] = bank
 
         def weigh(c, e):
@@ -196,18 +194,30 @@ def tile_attend_pkv8_sink_kernel(tc, qT, k_words, k_scales, v_words, v_scales, v
             nc.vector.tensor_tensor(
                 out=w_bf[c][:, e, :, :],
                 in0=turned[c, e][:].rearrange("p t q -> p q t"),
-                in1=vs_cols[:, g, :].unsqueeze(1).to_broadcast([P, P, PACK]),
+                in1=vs_cols[:, g, 0:PACK].unsqueeze(1).to_broadcast([P, P, PACK]),
                 op=ALU.mult,
             )
 
-        def weigh_on_scalar(c, e):
-            g = c // HALVES * PAGES + e
-            for t in range(PACK):
-                nc.scalar.activation(
-                    out=w_bf[c][:, e, :, t],
-                    in_=turned[c, e][:, t, :],
-                    func=ACT.Copy,
-                    scale=vs_cols[:, g, t : t + 1],
+        def weigh_on_scalar(c):
+            pairs = {}
+            for e in range(PAGES):
+                g = c // HALVES * PAGES + e
+                if c == 0:
+                    at = PROB_AT + (HALVES + e) * NEG_BYTES
+                    pairs[e] = turns.tile([P, 2, P, 2], BF16, name="pairs0_%d" % e, offset=at)
+                else:
+                    pairs[e] = keep.tile([P, 2, P, 2], BF16, name="pairs%d_%d" % (c, e))
+                for t in range(PACK):
+                    nc.scalar.activation(
+                        out=pairs[e][:, t // 2, :, t % 2],
+                        in_=turned[c, e][:, t, :],
+                        func=ACT.Copy,
+                        scale=vs_cols[:, g, t : t + 1],
+                    )
+            for e in range(PAGES):
+                nc.scalar.copy(
+                    out=w_bf[c][:, e, :, :].rearrange("p q t -> p (q t)").bitcast(F32).rearrange("p (q u) -> p q u", u=2),
+                    in_=pairs[e][:].rearrange("p u q i -> p (u q i)").bitcast(F32).rearrange("p (u q) -> p q u", u=2),
                 )
 
         def quantize_w(c, e0, e1):
@@ -220,7 +230,7 @@ def tile_attend_pkv8_sink_kernel(tc, qT, k_words, k_scales, v_words, v_scales, v
         def multiply(c, e):
             g = c // HALVES * PAGES + e
             if e == 0:
-                sums[c] = psum.tile([P, DV], F32, name="sums", tag="bank%d" % ((c + 1) % TILES))
+                sums[c] = psum.tile([P, DV], F32, name="sums", tag="bank%d" % SUM_BANK[c])
             nc.tensor.matmul_mx(
                 out=sums[c][:],
                 lhsT=w_codes[c][:, e, :].bitcast(FP8X4),
@@ -231,13 +241,10 @@ def tile_attend_pkv8_sink_kernel(tc, qT, k_words, k_scales, v_words, v_scales, v
                 stop=(e == PAGES - 1),
             )
 
-        def invert(c0, c1):
-            nc.vector.reciprocal(out=inverse[:, c0:c1], in_=total[:, c0:c1])
-
         def finish(c):
             b, h = divmod(c, HALVES)
             y = keep.tile([P, DV], F32, name="y%d" % c)
-            if c < HALVES:
+            if c < TILES - 1:
                 nc.scalar.activation(out=y[:], in_=sums[c][:], func=ACT.Copy, scale=inverse[:, c : c + 1])
             else:
                 nc.vector.tensor_scalar(
@@ -247,68 +254,70 @@ def tile_attend_pkv8_sink_kernel(tc, qT, k_words, k_scales, v_words, v_scales, v
 
         gather_keys(0)
         score(0, 0)
+        score(1, 0)
         gather_keys(1)
         score(0, 1)
-        score(1, 0)
-        gather_keys(2)
-        cast_q(1)
         score(1, 1)
         row_max(0, 0)
-        turn_vs(B * PAGES - 1, 0)
-        gather_keys(3)
-        q_codes.append(turns.tile([P, NQ], U32, name="q_codes1", align_bytes=64, offset=24576))
-        quantize_q(1)
-        score(2, 0)
-        score(3, 0)
-        score(2, 1)
-        score(3, 1)
+        row_max(1, 0)
         row_max(0, 1)
         exponentiate(0)
-        row_max(1, 0)
-        row_max(2, 0)
+        quantize_q(1)
+        gather_keys(2)
+        score(2, 0)
+        score(3, 0)
         row_max(1, 1)
         exponentiate(1)
+        gather_keys(3)
+        neg_max[1] = turns.tile([P, HALVES, PAGES], F32, name="neg_max1", offset=KW_POOL_AT)
         turn(0, 0)
         turn(0, 1)
+        score(2, 1)
+        score(3, 1)
+        turn(1, 0)
+        turn(1, 1)
+        weigh_on_scalar(0)
+        row_max(2, 0)
         row_max(3, 0)
         row_max(2, 1)
         exponentiate(2)
-        turn(1, 0)
         row_max(3, 1)
         exponentiate(3)
-        vw = turns.tile([P, B * PAGES * DV], U32, name="vw", align_bytes=64, offset=24576)
-        gather_values(0)
-        weigh(0, 0)
-        turn(1, 1)
+        weigh_on_scalar(1)
+        vw = turns.tile([P, B * PAGES * DV], U32, name="vw", align_bytes=64, offset=NEG_AT + 1024)
+        nc.vector.tensor_copy(vw[:], vw_pool[:].bitcast(U32).indirect(voffsets[:]))
+        vsc = turns.tile([P, B * PAGES * DV], U8, name="vsc", align_bytes=64, offset=NEG_AT)
+        nc.vector.tensor_copy(vsc[:], vsc_pool[:].bitcast(U8).indirect(voffsets[:]))
+        for c in range(HALVES, TILES):
+            at = VW_POOL_AT + 2048 * (c - HALVES)
+            w_bf[c] = turns.tile([P, PAGES, P, PACK], BF16, name="w_bf%d" % c, align_bytes=64, offset=at)
+        for c in range(HALVES):
+            at = VW_POOL_AT + 4096 + 1024 * c
+            w_codes[c] = turns.tile([P, PAGES, P], U32, name="w_codes%d" % c, align_bytes=64, offset=at)
+        inverse = turns.tile([P, TILES], F32, name="inverse", offset=VW_POOL_AT + 6144)
         turn(2, 0)
         turn(2, 1)
-        w_bf[2] = turns.tile([P, PAGES, P, PACK], BF16, name="w_bf2", align_bytes=64, offset=49152)
-        weigh_on_scalar(2, 0)
-        weigh_on_scalar(2, 1)
-        weigh(0, 1)
-        weigh(1, 0)
         turn(3, 0)
         turn(3, 1)
+        weigh(2, 0)
         quantize_w(0, 0, 2)
+        weigh(2, 1)
         multiply(0, 0)
         multiply(0, 1)
-        weigh(1, 1)
-        gather_values(1)
+        nc.vector.reciprocal(out=inverse[:], in_=total[:])
+        finish(0)
+        weigh(3, 0)
+        quantize_w(2, 0, 2)
+        multiply(2, 0)
+        multiply(2, 1)
+        quantize_w(3, 0, 1)
+        multiply(3, 0)
+        weigh(3, 1)
         quantize_w(1, 0, 2)
         multiply(1, 0)
         multiply(1, 1)
-        invert(0, 4)
-        finish(0)
-        finish(1)
-        weigh(3, 0)
-        quantize_w(2, 0, 1)
-        multiply(2, 0)
-        weigh(3, 1)
-        quantize_w(3, 0, 1)
-        multiply(3, 0)
         quantize_w(3, 1, 2)
         multiply(3, 1)
-        quantize_w(2, 1, 2)
-        multiply(2, 1)
-        finish(3)
         finish(2)
+        finish(1)
+        finish(3)

@@ -22,22 +22,24 @@ PACK = 4
 PAGES = N // PAGE
 TILES = B * NQ // P
 HALVES = NQ // P
-ROW = N + 8
+ROW = N + PACK
+PLANE = 264
 VS_ROW = P - 1
 V_PLANE = 4
-SCORE_BANK = {(0, 0): 0, (1, 0): 1, (0, 1): 2, (1, 1): 3, (2, 0): 4, (3, 0): 5, (2, 1): 6, (3, 1): 7}
-SUM_BANK = (5, 2, 4, 6)
+SCORE_BANK = {(c, e): 2 * c + e for c in range(TILES) for e in range(PAGES)}
+SUM_BANK = (1, 2, 4, 6)
 
 VS_AT = 2048
 KS_AT = 18432
 KW_POOL_AT = 24576
 Q_BF_AT = 40960
 NEG_AT = 49152
-NEG_BYTES = 4160
-VSC_AT = 66048
-PROB_AT = 68096
-IDENT_AT = 10240
-VW_POOL_AT = 10752
+NEG_BYTES = 4224
+VSC_AT = 86016
+FILL = -(2.0**120)
+PROB_AT = 66048
+IDENT_AT = 8192
+VW_POOL_AT = 10240
 
 
 def tile_attend_pkv8_sink_kernel(tc, qT, k_words, k_scales, v_words, v_scales, vs, sink, offs, voffs, out):
@@ -51,45 +53,46 @@ def tile_attend_pkv8_sink_kernel(tc, qT, k_words, k_scales, v_words, v_scales, v
         voffsets = keep.tile([P, B * PAGES * DV // 16], U16, name="voffsets")
         ks_pool = turns.tile([P, T // 4], I32, name="ks_pool", offset=KS_AT)
         vs_pool = turns.tile([P, T], F32, name="vs_pool", offset=VS_AT)
+        vsc_pool = turns.tile([P, T // PAGE * DV // 4], I32, name="vsc_pool", offset=VSC_AT)
         sink_rows = keep.tile([P, P], F32, name="sink_rows")
+        nc.vector.memset(vsc_pool[:], 0)
         nc.vector.memset(ks_pool[:], 0)
         nc.vector.memset(vs_pool[0:VS_ROW, :], 0.0)
-        vsc_pool = turns.tile([P, T // PAGE * DV // 4], I32, name="vsc_pool", offset=VSC_AT)
-        nc.vector.memset(vsc_pool[:], 0)
-        nc.gpsimd.memset(sink_rows[:], 0.0)
+        nc.gpsimd.memset(sink_rows[:], FILL)
 
-        nc.sync.dma_start(offsets[:], offs)
         nc.sync.dma_start(vs_pool[VS_ROW:P, :], vs[0:1, :])
         nc.sync.dma_start(voffsets[:], voffs)
-        nc.sync.dma_start(sink_rows[0:TILES, :], sink.rearrange("b (h p) o -> (b h) (p o)", p=P))
-        for r in range(4):
-            nc.sync.dma_start(ks_pool[r:P:32, :], k_scales[0, r:16:4, :].bitcast(I32))
-        q_raw = [keep.tile([P, PACK, NQ], F32, name="q_raw%d" % b) for b in range(B)]
-        kw_pool = turns.tile([P, T], I32, name="kw_pool", offset=KW_POOL_AT)
-        nc.sync.dma_start(q_raw[0][:], qT[0].rearrange("(p j) q -> p j q", j=PACK))
-        nc.sync.dma_start(kw_pool[:], k_words[0].rearrange("p t r -> p (t r)").bitcast(I32))
-        nc.sync.dma_start(q_raw[1][:], qT[1].rearrange("(p j) q -> p j q", j=PACK))
-
+        nc.sync.dma_start(offsets[:], offs)
         for r in range(4):
             nc.sync.dma_start(
                 vsc_pool[V_PLANE + r : P : 32, :].rearrange("f (u e) -> f u e", u=T // PAGE),
                 v_scales[:, r:16:4, :].rearrange("u f e -> f u e").bitcast(I32),
             )
+        for r in range(4):
+            nc.sync.dma_start(ks_pool[r:P:32, :], k_scales[0, r:16:4, :].bitcast(I32))
+        q_raw = [keep.tile([P, PACK, NQ], F32, name="q_raw%d" % b) for b in range(B)]
+        kw_pool = turns.tile([P, T], I32, name="kw_pool", offset=KW_POOL_AT)
+        nc.sync.dma_start(q_raw[0][:], qT[0].rearrange("(p j) q -> p j q", j=PACK))
+        nc.sync.dma_start(sink_rows[0 : TILES * PACK : PACK, :], sink.rearrange("b (h p) o -> (b h) (p o)", p=P))
+        nc.sync.dma_start(kw_pool[:], k_words[0].rearrange("p t r -> p (t r)").bitcast(I32))
+        nc.sync.dma_start(q_raw[1][:], qT[1].rearrange("(p j) q -> p j q", j=PACK))
 
         neg = [turns.tile([P, ROW], F32, name="neg%d" % c, offset=NEG_AT + c * NEG_BYTES) for c in range(TILES)]
 
-        vs_slots = keep.tile([P, B * N], F32, name="vs_slots")
+        vsc = keep.tile([P, B * PAGES * DV], U8, name="vsc", align_bytes=64)
+        nc.vector.tensor_copy(vsc[:], vsc_pool[:].bitcast(U8).indirect(voffsets[:]))
+        vs_slots = turns.tile([P, B * N], F32, name="vs_slots", offset=VSC_AT + 1024)
         nc.vector.tensor_copy(vs_slots[:], vs_pool[:].indirect(offsets[:]))
+        ident = turns.tile([P, P], F32, name="ident", offset=IDENT_AT)
+        make_identity(nc, ident[:])
         vs_cols = keep.tile([P, B * PAGES, 2 * PACK], F32, name="vs_cols")
         for g in range(B * PAGES):
             nc.sync.dma_start(
                 vs_cols[:, g, 0:PACK],
                 vs_slots[VS_ROW:P, g * PAGE : (g + 1) * PAGE].rearrange("o (p t) -> o p t", t=PACK),
             )
-        ident = turns.tile([P, P], F32, name="ident", offset=IDENT_AT)
-        make_identity(nc, ident[:])
 
-        ks = keep.tile([P, B * N], U8, name="ks", align_bytes=64)
+        ks = turns.tile([P, B * N], U8, name="ks", align_bytes=64, offset=VSC_AT - 1024)
         nc.vector.tensor_copy(ks[:], ks_pool[:].bitcast(U8).indirect(offsets[:]))
 
         vw_pool = turns.tile([P, T // PAGE * DV], I32, name="vw_pool", offset=VW_POOL_AT)
@@ -109,7 +112,7 @@ def tile_attend_pkv8_sink_kernel(tc, qT, k_words, k_scales, v_words, v_scales, v
             )
 
         def quantize_q(b):
-            q_codes[b] = turns.tile([P, NQ], U32, name="q_codes%d" % b, align_bytes=64, offset=9216)
+            q_codes[b] = turns.tile([P, NQ], U32, name="q_codes%d" % b, align_bytes=64, offset=(9216, KW_POOL_AT + 64)[b])
             nc.vector.quantize_mx(
                 out=q_codes[b][:].bitcast(FP8X4),
                 scales=q_scales[b][:],
@@ -122,20 +125,21 @@ def tile_attend_pkv8_sink_kernel(tc, qT, k_words, k_scales, v_words, v_scales, v
         sink_bank = psum.tile([P, P], F32, name="sink_bank", tag="bank7")
         nc.tensor.transpose(sink_bank[:], sink_rows[:], ident[:])
         for c in range(TILES):
-            nc.scalar.activation(out=neg[c][:, N : N + 1], in_=sink_bank[:, c : c + 1], func=ACT.Copy, scale=-1.0)
+            nc.scalar.activation(out=neg[c][:, N:ROW], in_=sink_bank[:, c * PACK : (c + 1) * PACK], func=ACT.Copy, scale=-1.0)
         cast_q(1)
 
         kw = {}
-        KW_AT = (VS_AT, VS_AT + 2048, VS_AT + 2048, NEG_AT)
-        neg_max = {0: keep.tile([P, HALVES, PAGES], F32, name="neg_max0")}
+        KW_AT = (KS_AT, KS_AT + 2048, VS_AT, VS_AT + 2048)
+        neg_max = [keep.tile([P, HALVES, PAGES], F32, name="neg_max%d" % b) for b in range(B)]
         total = keep.tile([P, TILES], F32, name="total")
         prob = {}
-        w_bf = {c: keep.tile([P, PAGES, P, PACK], BF16, name="w_bf%d" % c, align_bytes=64) for c in range(HALVES)}
-        w_codes = {c: keep.tile([P, PAGES, P], U32, name="w_codes%d" % c, align_bytes=64) for c in range(HALVES, TILES)}
+        w_bf = {c: keep.tile([P, PAGES, P, PACK], BF16, name="w_bf%d" % c, align_bytes=64) for c in range(TILES)}
+        w_codes = {c: keep.tile([P, PAGES, P], U32, name="w_codes%d" % c, align_bytes=64) for c in range(TILES)}
         w_scales = [keep.tile([P, PAGES, P], U8, name="w_scales%d" % c, align_bytes=64) for c in range(TILES)]
         scores = {}
         turned = {}
         sums = {}
+        planes = {}
 
         def gather_keys(g):
             kw[g] = turns.tile([P, PAGE], U32, name="kw%d" % g, align_bytes=64, offset=KW_AT[g])
@@ -162,8 +166,8 @@ def tile_attend_pkv8_sink_kernel(tc, qT, k_words, k_scales, v_words, v_scales, v
         def row_max(c, e):
             first = neg[c][:, N : N + 1] if e == 0 else neg_max[c // HALVES][:, c % HALVES, e - 1 : e]
             nc.vector.tensor_scalar(
-                out=neg[c][:, e * PAGE : (e + 1) * PAGE].rearrange("p (t s) -> p t s", t=PACK),
-                in0=scores[c, e][:].rearrange("p (s t) -> p t s", t=PACK),
+                out=neg[c][:, e * PAGE : (e + 1) * PAGE],
+                in0=scores[c, e][:],
                 scalar1=-1.0,
                 scalar2=first,
                 op0=ALU.mult,
@@ -172,10 +176,10 @@ def tile_attend_pkv8_sink_kernel(tc, qT, k_words, k_scales, v_words, v_scales, v
             )
 
         def exponentiate(c):
-            prob[c] = turns.tile([P, ROW], F32, name="prob%d" % c, offset=PROB_AT + c * NEG_BYTES)
+            prob[c] = turns.tile([P, PACK, PLANE], F32, name="prob%d" % c, offset=PROB_AT + c * NEG_BYTES)
             nc.scalar.activation(
-                out=prob[c][:, 0 : N + 1],
-                in_=neg[c][:, 0 : N + 1],
+                out=prob[c][:, :, 0 : ROW // PACK].rearrange("p t s -> p s t"),
+                in_=neg[c][:].rearrange("p (s t) -> p s t", t=PACK),
                 func=ACT.Exp,
                 scale=-1.0,
                 bias=neg_max[c // HALVES][:, c % HALVES, PAGES - 1 : PAGES],
@@ -185,8 +189,7 @@ def tile_attend_pkv8_sink_kernel(tc, qT, k_words, k_scales, v_words, v_scales, v
         def turn(c, e):
             bank = psum.tile([P, PACK, P], F32, name="turned", tag="bank%d" % (c * PAGES + e))
             for t in range(PACK):
-                first = e * PAGE + t * P
-                nc.tensor.transpose(bank[:, t, :], prob[c][:, first : first + P], ident[:])
+                nc.tensor.transpose(bank[:, t, :], prob[c][:, t, e * P : (e + 1) * P], ident[:])
             turned[c, e] = bank
 
         def weigh(c, e):
@@ -198,27 +201,22 @@ def tile_attend_pkv8_sink_kernel(tc, qT, k_words, k_scales, v_words, v_scales, v
                 op=ALU.mult,
             )
 
-        def weigh_on_scalar(c):
-            pairs = {}
-            for e in range(PAGES):
-                g = c // HALVES * PAGES + e
-                if c == 0:
-                    at = PROB_AT + (HALVES + e) * NEG_BYTES
-                    pairs[e] = turns.tile([P, 2, P, 2], BF16, name="pairs0_%d" % e, offset=at)
-                else:
-                    pairs[e] = keep.tile([P, 2, P, 2], BF16, name="pairs%d_%d" % (c, e))
-                for t in range(PACK):
-                    nc.scalar.activation(
-                        out=pairs[e][:, t // 2, :, t % 2],
-                        in_=turned[c, e][:, t, :],
-                        func=ACT.Copy,
-                        scale=vs_cols[:, g, t : t + 1],
-                    )
-            for e in range(PAGES):
-                nc.scalar.copy(
-                    out=w_bf[c][:, e, :, :].rearrange("p q t -> p (q t)").bitcast(F32).rearrange("p (q u) -> p q u", u=2),
-                    in_=pairs[e][:].rearrange("p u q i -> p (u q i)").bitcast(F32).rearrange("p (u q) -> p q u", u=2),
+        def scale_planes(c, e, at):
+            g = c // HALVES * PAGES + e
+            planes[c, e] = turns.tile([P, PACK, P], BF16, name="planes%d_%d" % (c, e), offset=at)
+            for t in range(PACK):
+                nc.scalar.activation(
+                    out=planes[c, e][:, t, :],
+                    in_=turned[c, e][:, t, :],
+                    func=ACT.Copy,
+                    scale=vs_cols[:, g, t : t + 1],
                 )
+
+        def weave(c, e):
+            nc.scalar.copy(
+                out=w_bf[c][:, e, :, :].rearrange("p (k i) t -> p k t i", i=4),
+                in_=planes[c, e][:].rearrange("p t (k i) -> p k t i", i=4),
+            )
 
         def quantize_w(c, e0, e1):
             nc.vector.quantize_mx(
@@ -227,9 +225,9 @@ def tile_attend_pkv8_sink_kernel(tc, qT, k_words, k_scales, v_words, v_scales, v
                 in_=w_bf[c][:, e0:e1, :, :].rearrange("p e q t -> p (e q t)"),
             )
 
-        def multiply(c, e):
+        def multiply(c, e, first):
             g = c // HALVES * PAGES + e
-            if e == 0:
+            if first:
                 sums[c] = psum.tile([P, DV], F32, name="sums", tag="bank%d" % SUM_BANK[c])
             nc.tensor.matmul_mx(
                 out=sums[c][:],
@@ -237,14 +235,14 @@ def tile_attend_pkv8_sink_kernel(tc, qT, k_words, k_scales, v_words, v_scales, v
                 lhsT_scale=w_scales[c][:, e, :],
                 rhs=vw[:, g * DV : (g + 1) * DV].bitcast(FP8X4),
                 rhs_scale=vsc[V_PLANE:P, g * DV : (g + 1) * DV],
-                start=(e == 0),
-                stop=(e == PAGES - 1),
+                start=first,
+                stop=not first,
             )
 
         def finish(c):
             b, h = divmod(c, HALVES)
             y = keep.tile([P, DV], F32, name="y%d" % c)
-            if c < TILES - 1:
+            if c != 2:
                 nc.scalar.activation(out=y[:], in_=sums[c][:], func=ACT.Copy, scale=inverse[:, c : c + 1])
             else:
                 nc.vector.tensor_scalar(
@@ -254,70 +252,65 @@ def tile_attend_pkv8_sink_kernel(tc, qT, k_words, k_scales, v_words, v_scales, v
 
         gather_keys(0)
         score(0, 0)
-        score(1, 0)
         gather_keys(1)
         score(0, 1)
+        score(1, 0)
+        gather_keys(2)
         score(1, 1)
         row_max(0, 0)
+        gather_keys(3)
         row_max(1, 0)
-        row_max(0, 1)
-        exponentiate(0)
         quantize_q(1)
-        gather_keys(2)
         score(2, 0)
         score(3, 0)
-        row_max(1, 1)
-        exponentiate(1)
-        gather_keys(3)
-        neg_max[1] = turns.tile([P, HALVES, PAGES], F32, name="neg_max1", offset=KW_POOL_AT)
-        turn(0, 0)
-        turn(0, 1)
         score(2, 1)
         score(3, 1)
-        turn(1, 0)
-        turn(1, 1)
-        weigh_on_scalar(0)
+        row_max(0, 1)
+        exponentiate(0)
         row_max(2, 0)
+        row_max(1, 1)
+        exponentiate(1)
+        turn(0, 0)
+        turn(0, 1)
         row_max(3, 0)
         row_max(2, 1)
         exponentiate(2)
+        turn(1, 0)
+        turn(1, 1)
         row_max(3, 1)
         exponentiate(3)
-        weigh_on_scalar(1)
-        vw = turns.tile([P, B * PAGES * DV], U32, name="vw", align_bytes=64, offset=NEG_AT + 1024)
+        vw = turns.tile([P, B * PAGES * DV], U32, name="vw", align_bytes=64, offset=VS_AT + 2048)
         nc.vector.tensor_copy(vw[:], vw_pool[:].bitcast(U32).indirect(voffsets[:]))
-        vsc = turns.tile([P, B * PAGES * DV], U8, name="vsc", align_bytes=64, offset=NEG_AT)
-        nc.vector.tensor_copy(vsc[:], vsc_pool[:].bitcast(U8).indirect(voffsets[:]))
-        for c in range(HALVES, TILES):
-            at = VW_POOL_AT + 2048 * (c - HALVES)
-            w_bf[c] = turns.tile([P, PAGES, P, PACK], BF16, name="w_bf%d" % c, align_bytes=64, offset=at)
-        for c in range(HALVES):
-            at = VW_POOL_AT + 4096 + 1024 * c
-            w_codes[c] = turns.tile([P, PAGES, P], U32, name="w_codes%d" % c, align_bytes=64, offset=at)
-        inverse = turns.tile([P, TILES], F32, name="inverse", offset=VW_POOL_AT + 6144)
+        inverse = turns.tile([P, TILES], F32, name="inverse", offset=VW_POOL_AT)
         turn(2, 0)
         turn(2, 1)
         turn(3, 0)
         turn(3, 1)
-        weigh(2, 0)
+        scale_planes(2, 0, NEG_AT + 2 * NEG_BYTES)
+        scale_planes(2, 1, NEG_AT + 2 * NEG_BYTES + 1024)
+        weave(2, 0)
+        weave(2, 1)
+        weigh(0, 0)
+        weigh(0, 1)
+        weigh(1, 0)
         quantize_w(0, 0, 2)
-        weigh(2, 1)
-        multiply(0, 0)
-        multiply(0, 1)
-        nc.vector.reciprocal(out=inverse[:], in_=total[:])
-        finish(0)
+        multiply(0, 0, True)
+        multiply(0, 1, False)
+        weigh(1, 1)
         weigh(3, 0)
-        quantize_w(2, 0, 2)
-        multiply(2, 0)
-        multiply(2, 1)
-        quantize_w(3, 0, 1)
-        multiply(3, 0)
-        weigh(3, 1)
+        nc.vector.reciprocal(out=inverse[:], in_=total[:])
         quantize_w(1, 0, 2)
-        multiply(1, 0)
-        multiply(1, 1)
-        quantize_w(3, 1, 2)
-        multiply(3, 1)
-        finish(2)
+        multiply(1, 0, True)
+        multiply(1, 1, False)
+        finish(0)
         finish(1)
+        weigh(3, 1)
+        quantize_w(3, 0, 1)
+        multiply(3, 0, True)
+        quantize_w(2, 0, 2)
+        quantize_w(3, 1, 2)
+        multiply(3, 1, False)
+        multiply(2, 0, True)
+        multiply(2, 1, False)
         finish(3)
+        finish(2)

@@ -26,20 +26,23 @@ ROW = N + PACK
 PLANE = 264
 VS_ROW = P - 1
 V_PLANE = 4
-SCORE_BANK = {(c, e): 2 * c + e for c in range(TILES) for e in range(PAGES)}
-SUM_BANK = (1, 2, 4, 6)
-
-VS_AT = 2048
-KS_AT = 18432
-KW_POOL_AT = 24576
-Q_BF_AT = 40960
-NEG_AT = 49152
-NEG_BYTES = 4224
-VSC_AT = 86016
+SCORE_BANK = {(0, 0): 0, (0, 1): 1, (1, 0): 2, (1, 1): 3, (2, 0): 4, (3, 0): 5, (2, 1): 6, (3, 1): 7}
+TURN_BANK = {(0, 0): 0, (0, 1): 1, (1, 0): 5, (1, 1): 6, (2, 0): 2, (2, 1): 4, (3, 0): 3, (3, 1): 7}
+SUM_BANK = (2, 4, 0, 1)
+SINK_ROW = P - TILES
 FILL = -(2.0**120)
-PROB_AT = 66048
-IDENT_AT = 8192
-VW_POOL_AT = 10240
+
+VS_AT = 0
+IDENT_AT = VS_AT
+Q0_CODES_AT = 76800
+KS_AT = 16384
+VSC_POOL_AT = VS_AT + 1024
+VW_POOL_AT = KS_AT - 4096
+KW_POOL_AT = 20480
+NEG_AT = 36864
+NEG_BYTES = 4224
+PROB_AT = NEG_AT + TILES * NEG_BYTES
+KW_AT = (70656, 72704, 74752, NEG_AT)
 
 
 def tile_attend_pkv8_sink_kernel(tc, qT, k_words, k_scales, v_words, v_scales, vs, sink, offs, voffs, out):
@@ -53,35 +56,26 @@ def tile_attend_pkv8_sink_kernel(tc, qT, k_words, k_scales, v_words, v_scales, v
         voffsets = keep.tile([P, B * PAGES * DV // 16], U16, name="voffsets")
         ks_pool = turns.tile([P, T // 4], I32, name="ks_pool", offset=KS_AT)
         vs_pool = turns.tile([P, T], F32, name="vs_pool", offset=VS_AT)
-        vsc_pool = turns.tile([P, T // PAGE * DV // 4], I32, name="vsc_pool", offset=VSC_AT)
         sink_rows = keep.tile([P, P], F32, name="sink_rows")
-        nc.vector.memset(vsc_pool[:], 0)
         nc.vector.memset(ks_pool[:], 0)
         nc.vector.memset(vs_pool[0:VS_ROW, :], 0.0)
-        nc.gpsimd.memset(sink_rows[:], FILL)
+        nc.gpsimd.memset(sink_rows[0:SINK_ROW, :], FILL)
 
-        nc.sync.dma_start(vs_pool[VS_ROW:P, :], vs[0:1, :])
-        nc.sync.dma_start(voffsets[:], voffs)
-        nc.sync.dma_start(offsets[:], offs)
-        for r in range(4):
-            nc.sync.dma_start(
-                vsc_pool[V_PLANE + r : P : 32, :].rearrange("f (u e) -> f u e", u=T // PAGE),
-                v_scales[:, r:16:4, :].rearrange("u f e -> f u e").bitcast(I32),
-            )
-        for r in range(4):
-            nc.sync.dma_start(ks_pool[r:P:32, :], k_scales[0, r:16:4, :].bitcast(I32))
         q_raw = [keep.tile([P, PACK, NQ], F32, name="q_raw%d" % b) for b in range(B)]
         kw_pool = turns.tile([P, T], I32, name="kw_pool", offset=KW_POOL_AT)
+        nc.sync.dma_start(vs_pool[VS_ROW:P, :], vs[0:1, :])
+        nc.sync.dma_start(offsets[:], offs)
+        nc.sync.dma_start(sink_rows[SINK_ROW:P, :], sink.rearrange("b (h p) o -> (b h) (p o)", p=P))
         nc.sync.dma_start(q_raw[0][:], qT[0].rearrange("(p j) q -> p j q", j=PACK))
-        nc.sync.dma_start(sink_rows[0 : TILES * PACK : PACK, :], sink.rearrange("b (h p) o -> (b h) (p o)", p=P))
+        for r in range(4):
+            nc.sync.dma_start(ks_pool[r:P:32, :], k_scales[0, r:16:4, :].bitcast(I32))
         nc.sync.dma_start(kw_pool[:], k_words[0].rearrange("p t r -> p (t r)").bitcast(I32))
         nc.sync.dma_start(q_raw[1][:], qT[1].rearrange("(p j) q -> p j q", j=PACK))
+        nc.sync.dma_start(voffsets[:], voffs)
 
         neg = [turns.tile([P, ROW], F32, name="neg%d" % c, offset=NEG_AT + c * NEG_BYTES) for c in range(TILES)]
 
-        vsc = keep.tile([P, B * PAGES * DV], U8, name="vsc", align_bytes=64)
-        nc.vector.tensor_copy(vsc[:], vsc_pool[:].bitcast(U8).indirect(voffsets[:]))
-        vs_slots = turns.tile([P, B * N], F32, name="vs_slots", offset=VSC_AT + 1024)
+        vs_slots = keep.tile([P, B * N], F32, name="vs_slots")
         nc.vector.tensor_copy(vs_slots[:], vs_pool[:].indirect(offsets[:]))
         ident = turns.tile([P, P], F32, name="ident", offset=IDENT_AT)
         make_identity(nc, ident[:])
@@ -92,16 +86,16 @@ def tile_attend_pkv8_sink_kernel(tc, qT, k_words, k_scales, v_words, v_scales, v
                 vs_slots[VS_ROW:P, g * PAGE : (g + 1) * PAGE].rearrange("o (p t) -> o p t", t=PACK),
             )
 
-        ks = turns.tile([P, B * N], U8, name="ks", align_bytes=64, offset=VSC_AT - 1024)
+        ks = keep.tile([P, B * N], U8, name="ks", align_bytes=64)
         nc.vector.tensor_copy(ks[:], ks_pool[:].bitcast(U8).indirect(offsets[:]))
 
         vw_pool = turns.tile([P, T // PAGE * DV], I32, name="vw_pool", offset=VW_POOL_AT)
-        nc.sync.dma_start(
+        nc.scalar.dma_start(
             vw_pool[:].rearrange("p (u e) -> p u e", e=DV),
             v_words.rearrange("u p e r -> p u (e r)").bitcast(I32),
         )
 
-        q_bf = [turns.tile([P, NQ, PACK], BF16, name="q_bf%d" % b, align_bytes=64, offset=Q_BF_AT + 2048 * b) for b in range(B)]
+        q_bf = [keep.tile([P, NQ, PACK], BF16, name="q_bf%d" % b, align_bytes=64) for b in range(B)]
         q_codes = {}
         q_scales = [keep.tile([P, NQ], U8, name="q_scales%d" % b, align_bytes=64) for b in range(B)]
 
@@ -112,7 +106,7 @@ def tile_attend_pkv8_sink_kernel(tc, qT, k_words, k_scales, v_words, v_scales, v
             )
 
         def quantize_q(b):
-            q_codes[b] = turns.tile([P, NQ], U32, name="q_codes%d" % b, align_bytes=64, offset=(9216, KW_POOL_AT + 64)[b])
+            q_codes[b] = turns.tile([P, NQ], U32, name="q_codes%d" % b, align_bytes=64, offset=(Q0_CODES_AT, KW_AT[0])[b])
             nc.vector.quantize_mx(
                 out=q_codes[b][:].bitcast(FP8X4),
                 scales=q_scales[b][:],
@@ -122,19 +116,26 @@ def tile_attend_pkv8_sink_kernel(tc, qT, k_words, k_scales, v_words, v_scales, v
         cast_q(0)
         quantize_q(0)
 
+        vsc_pool = turns.tile([P, T // PAGE * DV // 4], I32, name="vsc_pool", offset=VSC_POOL_AT)
+        nc.gpsimd.memset(vsc_pool[:], 0)
+        for r in range(4):
+            nc.sync.dma_start(
+                vsc_pool[V_PLANE + r : P : 32, :].rearrange("f (u e) -> f u e", u=T // PAGE),
+                v_scales[:, r:16:4, :].rearrange("u f e -> f u e").bitcast(I32),
+            )
+
         sink_bank = psum.tile([P, P], F32, name="sink_bank", tag="bank7")
         nc.tensor.transpose(sink_bank[:], sink_rows[:], ident[:])
         for c in range(TILES):
-            nc.scalar.activation(out=neg[c][:, N:ROW], in_=sink_bank[:, c * PACK : (c + 1) * PACK], func=ACT.Copy, scale=-1.0)
+            nc.scalar.activation(out=neg[c][:, N:ROW], in_=sink_bank[:, SINK_ROW + c - 3 * TILES : P : TILES], func=ACT.Copy, scale=-1.0)
         cast_q(1)
 
         kw = {}
-        KW_AT = (KS_AT, KS_AT + 2048, VS_AT, VS_AT + 2048)
         neg_max = [keep.tile([P, HALVES, PAGES], F32, name="neg_max%d" % b) for b in range(B)]
         total = keep.tile([P, TILES], F32, name="total")
         prob = {}
         w_bf = {c: keep.tile([P, PAGES, P, PACK], BF16, name="w_bf%d" % c, align_bytes=64) for c in range(TILES)}
-        w_codes = {c: keep.tile([P, PAGES, P], U32, name="w_codes%d" % c, align_bytes=64) for c in range(TILES)}
+        w_codes = {c: keep.tile([P, PAGES, P], U32, name="w_codes%d" % c, align_bytes=64) for c in range(TILES) if c != 1}
         w_scales = [keep.tile([P, PAGES, P], U8, name="w_scales%d" % c, align_bytes=64) for c in range(TILES)]
         scores = {}
         turned = {}
@@ -164,7 +165,7 @@ def tile_attend_pkv8_sink_kernel(tc, qT, k_words, k_scales, v_words, v_scales, v
             scores[c, e] = bank
 
         def row_max(c, e):
-            first = neg[c][:, N : N + 1] if e == 0 else neg_max[c // HALVES][:, c % HALVES, e - 1 : e]
+            first = neg[c][:, ROW - 1 : ROW] if e == 0 else neg_max[c // HALVES][:, c % HALVES, e - 1 : e]
             nc.vector.tensor_scalar(
                 out=neg[c][:, e * PAGE : (e + 1) * PAGE],
                 in0=scores[c, e][:],
@@ -187,7 +188,7 @@ def tile_attend_pkv8_sink_kernel(tc, qT, k_words, k_scales, v_words, v_scales, v
             )
 
         def turn(c, e):
-            bank = psum.tile([P, PACK, P], F32, name="turned", tag="bank%d" % (c * PAGES + e))
+            bank = psum.tile([P, PACK, P], F32, name="turned", tag="bank%d" % TURN_BANK[c, e])
             for t in range(PACK):
                 nc.tensor.transpose(bank[:, t, :], prob[c][:, t, e * P : (e + 1) * P], ident[:])
             turned[c, e] = bank
@@ -201,9 +202,9 @@ def tile_attend_pkv8_sink_kernel(tc, qT, k_words, k_scales, v_words, v_scales, v
                 op=ALU.mult,
             )
 
-        def scale_planes(c, e, at):
+        def scale_planes(c, e):
             g = c // HALVES * PAGES + e
-            planes[c, e] = turns.tile([P, PACK, P], BF16, name="planes%d_%d" % (c, e), offset=at)
+            planes[c, e] = keep.tile([P, PACK, P], BF16, name="planes%d_%d" % (c, e))
             for t in range(PACK):
                 nc.scalar.activation(
                     out=planes[c, e][:, t, :],
@@ -242,7 +243,7 @@ def tile_attend_pkv8_sink_kernel(tc, qT, k_words, k_scales, v_words, v_scales, v
         def finish(c):
             b, h = divmod(c, HALVES)
             y = keep.tile([P, DV], F32, name="y%d" % c)
-            if c != 2:
+            if c != TILES - 1:
                 nc.scalar.activation(out=y[:], in_=sums[c][:], func=ACT.Copy, scale=inverse[:, c : c + 1])
             else:
                 nc.vector.tensor_scalar(
@@ -253,64 +254,70 @@ def tile_attend_pkv8_sink_kernel(tc, qT, k_words, k_scales, v_words, v_scales, v
         gather_keys(0)
         score(0, 0)
         gather_keys(1)
-        score(0, 1)
         score(1, 0)
-        gather_keys(2)
+        score(0, 1)
         score(1, 1)
+        gather_keys(2)
         row_max(0, 0)
-        gather_keys(3)
         row_max(1, 0)
+        row_max(0, 1)
+        exponentiate(0)
         quantize_q(1)
         score(2, 0)
         score(3, 0)
-        score(2, 1)
-        score(3, 1)
-        row_max(0, 1)
-        exponentiate(0)
-        row_max(2, 0)
         row_max(1, 1)
         exponentiate(1)
         turn(0, 0)
         turn(0, 1)
+        row_max(2, 0)
+        gather_keys(3)
+        score(2, 1)
+        score(3, 1)
+        scale_planes(0, 0)
+        scale_planes(0, 1)
         row_max(3, 0)
         row_max(2, 1)
-        exponentiate(2)
         turn(1, 0)
         turn(1, 1)
+        exponentiate(2)
         row_max(3, 1)
         exponentiate(3)
-        vw = turns.tile([P, B * PAGES * DV], U32, name="vw", align_bytes=64, offset=VS_AT + 2048)
-        nc.vector.tensor_copy(vw[:], vw_pool[:].bitcast(U32).indirect(voffsets[:]))
-        inverse = turns.tile([P, TILES], F32, name="inverse", offset=VW_POOL_AT)
         turn(2, 0)
         turn(2, 1)
         turn(3, 0)
         turn(3, 1)
-        scale_planes(2, 0, NEG_AT + 2 * NEG_BYTES)
-        scale_planes(2, 1, NEG_AT + 2 * NEG_BYTES + 1024)
+        weave(0, 0)
+        weave(0, 1)
+        scale_planes(2, 0)
+        scale_planes(2, 1)
         weave(2, 0)
         weave(2, 1)
-        weigh(0, 0)
-        weigh(0, 1)
+        vsc = turns.tile([P, B * PAGES * DV], U8, name="vsc", align_bytes=64, offset=KW_AT[3])
+        nc.vector.tensor_copy(vsc[:], vsc_pool[:].bitcast(U8).indirect(voffsets[:]))
+        vw = turns.tile([P, B * PAGES * DV], U32, name="vw", align_bytes=64, offset=KW_AT[3] + 1024)
+        nc.vector.tensor_copy(vw[:], vw_pool[:].bitcast(U32).indirect(voffsets[:]))
+        inverse = keep.tile([P, TILES], F32, name="inverse")
         weigh(1, 0)
+        weigh(1, 1)
         quantize_w(0, 0, 2)
         multiply(0, 0, True)
         multiply(0, 1, False)
-        weigh(1, 1)
-        weigh(3, 0)
         nc.vector.reciprocal(out=inverse[:], in_=total[:])
+        weigh(3, 0)
+        w_codes[1] = turns.tile([P, PAGES, P], U32, name="w_codes1", align_bytes=64, offset=PROB_AT + 3 * NEG_BYTES)
         quantize_w(1, 0, 2)
         multiply(1, 0, True)
         multiply(1, 1, False)
         finish(0)
         finish(1)
-        weigh(3, 1)
         quantize_w(3, 0, 1)
         multiply(3, 0, True)
-        quantize_w(2, 0, 2)
-        quantize_w(3, 1, 2)
-        multiply(3, 1, False)
+        quantize_w(2, 0, 1)
         multiply(2, 0, True)
+        weigh(3, 1)
+        quantize_w(2, 1, 2)
+        quantize_w(3, 1, 2)
         multiply(2, 1, False)
-        finish(3)
+        multiply(3, 1, False)
         finish(2)
+        finish(3)

@@ -26,23 +26,24 @@ ROW = N + PACK
 PLANE = 264
 VS_ROW = P - 1
 V_PLANE = 4
-SCORE_BANK = {(0, 0): 0, (0, 1): 1, (1, 0): 2, (1, 1): 3, (2, 0): 4, (3, 0): 5, (2, 1): 6, (3, 1): 7}
-TURN_BANK = {(0, 0): 0, (0, 1): 1, (1, 0): 5, (1, 1): 6, (2, 0): 2, (2, 1): 4, (3, 0): 3, (3, 1): 7}
-SUM_BANK = (2, 4, 0, 1)
+SCORE_BANK = {(c, e): 2 * c + e for c in range(TILES) for e in range(PAGES)}
+SUM_BANK = (4, 5, 0, 1)
 SINK_ROW = P - TILES
 FILL = -(2.0**120)
 
 VS_AT = 0
-IDENT_AT = VS_AT
-Q0_CODES_AT = 76800
+Q0_CODES_AT = 83968
+Q0_RAW_AT = 86016
+KS_ROW = P - 16
+VS_EARLY = 2816
+SINK_AT = 102400
 KS_AT = 16384
-VSC_POOL_AT = VS_AT + 1024
-VW_POOL_AT = KS_AT - 4096
+VW_POOL_AT = 75776
 KW_POOL_AT = 20480
 NEG_AT = 36864
 NEG_BYTES = 4224
 PROB_AT = NEG_AT + TILES * NEG_BYTES
-KW_AT = (70656, 72704, 74752, NEG_AT)
+KW_AT = (74752, 70656, 72704, 70656)
 
 
 def tile_attend_pkv8_sink_kernel(tc, qT, k_words, k_scales, v_words, v_scales, vs, sink, offs, voffs, out):
@@ -56,50 +57,36 @@ def tile_attend_pkv8_sink_kernel(tc, qT, k_words, k_scales, v_words, v_scales, v
         voffsets = keep.tile([P, B * PAGES * DV // 16], U16, name="voffsets")
         ks_pool = turns.tile([P, T // 4], I32, name="ks_pool", offset=KS_AT)
         vs_pool = turns.tile([P, T], F32, name="vs_pool", offset=VS_AT)
-        sink_rows = keep.tile([P, P], F32, name="sink_rows")
-        nc.vector.memset(ks_pool[:], 0)
-        nc.vector.memset(vs_pool[0:VS_ROW, :], 0.0)
+        sink_rows = turns.tile([P, P], F32, name="sink_rows", offset=SINK_AT)
+        nc.vector.memset(ks_pool[0:KS_ROW, :], 0)
+        ks = keep.tile([P, B * N], U8, name="ks", align_bytes=64)
+        nc.vector.memset(ks[:].bitcast(I32), 0)
+        nc.vector.memset(vs_pool[0:VS_ROW, 0:VS_EARLY], 0.0)
         nc.gpsimd.memset(sink_rows[0:SINK_ROW, :], FILL)
 
-        q_raw = [keep.tile([P, PACK, NQ], F32, name="q_raw%d" % b) for b in range(B)]
+        q_raw = [turns.tile([P, PACK, NQ], F32, name="q_raw%d" % b, offset=Q0_RAW_AT + 8192 * b) for b in range(B)]
         kw_pool = turns.tile([P, T], I32, name="kw_pool", offset=KW_POOL_AT)
-        nc.sync.dma_start(vs_pool[VS_ROW:P, :], vs[0:1, :])
         nc.sync.dma_start(offsets[:], offs)
-        nc.sync.dma_start(sink_rows[SINK_ROW:P, :], sink.rearrange("b (h p) o -> (b h) (p o)", p=P))
+        nc.sync.dma_start(ks_pool[KS_ROW:P, :], k_scales[0].bitcast(I32))
         nc.sync.dma_start(q_raw[0][:], qT[0].rearrange("(p j) q -> p j q", j=PACK))
-        for r in range(4):
-            nc.sync.dma_start(ks_pool[r:P:32, :], k_scales[0, r:16:4, :].bitcast(I32))
+        nc.sync.dma_start(sink_rows[SINK_ROW:P, :], sink.rearrange("b (h p) o -> (b h) (p o)", p=P))
+        nc.sync.dma_start(vs_pool[VS_ROW:P, :], vs[0:1, :])
         nc.sync.dma_start(kw_pool[:], k_words[0].rearrange("p t r -> p (t r)").bitcast(I32))
         nc.sync.dma_start(q_raw[1][:], qT[1].rearrange("(p j) q -> p j q", j=PACK))
         nc.sync.dma_start(voffsets[:], voffs)
 
         neg = [turns.tile([P, ROW], F32, name="neg%d" % c, offset=NEG_AT + c * NEG_BYTES) for c in range(TILES)]
 
-        vs_slots = keep.tile([P, B * N], F32, name="vs_slots")
-        nc.vector.tensor_copy(vs_slots[:], vs_pool[:].indirect(offsets[:]))
-        ident = turns.tile([P, P], F32, name="ident", offset=IDENT_AT)
-        make_identity(nc, ident[:])
-        vs_cols = keep.tile([P, B * PAGES, 2 * PACK], F32, name="vs_cols")
-        for g in range(B * PAGES):
-            nc.sync.dma_start(
-                vs_cols[:, g, 0:PACK],
-                vs_slots[VS_ROW:P, g * PAGE : (g + 1) * PAGE].rearrange("o (p t) -> o p t", t=PACK),
-            )
+        ks_rows = keep.tile([P, B * N], U8, name="ks_rows", align_bytes=64)
+        nc.vector.tensor_copy(ks_rows[:], ks_pool[:].bitcast(U8).indirect(offsets[:]))
+        nc.vector.memset(vs_pool[0:VS_ROW, VS_EARLY:T], 0.0)
 
-        ks = keep.tile([P, B * N], U8, name="ks", align_bytes=64)
-        nc.vector.tensor_copy(ks[:], ks_pool[:].bitcast(U8).indirect(offsets[:]))
-
-        vw_pool = turns.tile([P, T // PAGE * DV], I32, name="vw_pool", offset=VW_POOL_AT)
-        nc.scalar.dma_start(
-            vw_pool[:].rearrange("p (u e) -> p u e", e=DV),
-            v_words.rearrange("u p e r -> p u (e r)").bitcast(I32),
-        )
-
-        q_bf = [keep.tile([P, NQ, PACK], BF16, name="q_bf%d" % b, align_bytes=64) for b in range(B)]
+        q_bf = {}
         q_codes = {}
         q_scales = [keep.tile([P, NQ], U8, name="q_scales%d" % b, align_bytes=64) for b in range(B)]
 
         def cast_q(b):
+            q_bf[b] = turns.tile([P, NQ, PACK], BF16, name="q_bf%d" % b, align_bytes=64, offset=(SINK_AT + 2048, SINK_AT)[b])
             nc.scalar.copy(
                 out=q_bf[b][:].rearrange("p (c i) j -> p c j i", i=4),
                 in_=q_raw[b][:].rearrange("p j (c i) -> p c j i", i=4),
@@ -116,7 +103,26 @@ def tile_attend_pkv8_sink_kernel(tc, qT, k_words, k_scales, v_words, v_scales, v
         cast_q(0)
         quantize_q(0)
 
-        vsc_pool = turns.tile([P, T // PAGE * DV // 4], I32, name="vsc_pool", offset=VSC_POOL_AT)
+        ident = turns.tile([P, P], F32, name="ident", offset=Q0_RAW_AT + 2048)
+        make_identity(nc, ident[:])
+        for c in range(TILES):
+            sink_bank = psum.tile([P, P], F32, name="sink_bank", tag="bank%d" % c)
+            nc.tensor.transpose(sink_bank[:], sink_rows[:], ident[:])
+            nc.scalar.activation(out=neg[c][:, N:ROW], in_=sink_bank[:, SINK_ROW + c - 3 * TILES : P : TILES], func=ACT.Copy, scale=-1.0)
+
+        for r in range(4):
+            nc.scalar.dma_start(ks[r:P:32, :].bitcast(I32), ks_rows[KS_ROW + r : P : 4, :].bitcast(I32))
+
+        vs_slots = keep.tile([P, B * N], F32, name="vs_slots")
+        nc.vector.tensor_copy(vs_slots[:], vs_pool[:].indirect(offsets[:]))
+        vs_cols = keep.tile([P, B * PAGES, 2 * PACK], F32, name="vs_cols")
+        for g in range(B * PAGES):
+            nc.sync.dma_start(
+                vs_cols[:, g, 0:PACK],
+                vs_slots[VS_ROW:P, g * PAGE : (g + 1) * PAGE].rearrange("o (p t) -> o p t", t=PACK),
+            )
+
+        vsc_pool = turns.tile([P, T // PAGE * DV // 4], I32, name="vsc_pool", offset=Q0_RAW_AT + 2560)
         nc.gpsimd.memset(vsc_pool[:], 0)
         for r in range(4):
             nc.sync.dma_start(
@@ -124,10 +130,6 @@ def tile_attend_pkv8_sink_kernel(tc, qT, k_words, k_scales, v_words, v_scales, v
                 v_scales[:, r:16:4, :].rearrange("u f e -> f u e").bitcast(I32),
             )
 
-        sink_bank = psum.tile([P, P], F32, name="sink_bank", tag="bank7")
-        nc.tensor.transpose(sink_bank[:], sink_rows[:], ident[:])
-        for c in range(TILES):
-            nc.scalar.activation(out=neg[c][:, N:ROW], in_=sink_bank[:, SINK_ROW + c - 3 * TILES : P : TILES], func=ACT.Copy, scale=-1.0)
         cast_q(1)
 
         kw = {}
@@ -188,7 +190,7 @@ def tile_attend_pkv8_sink_kernel(tc, qT, k_words, k_scales, v_words, v_scales, v
             )
 
         def turn(c, e):
-            bank = psum.tile([P, PACK, P], F32, name="turned", tag="bank%d" % TURN_BANK[c, e])
+            bank = psum.tile([P, PACK, P], F32, name="turned", tag="bank%d" % SCORE_BANK[c, e])
             for t in range(PACK):
                 nc.tensor.transpose(bank[:, t, :], prob[c][:, t, e * P : (e + 1) * P], ident[:])
             turned[c, e] = bank
@@ -253,10 +255,15 @@ def tile_attend_pkv8_sink_kernel(tc, qT, k_words, k_scales, v_words, v_scales, v
 
         gather_keys(0)
         score(0, 0)
-        gather_keys(1)
         score(1, 0)
+        gather_keys(1)
         score(0, 1)
         score(1, 1)
+        vw_pool = turns.tile([P, T // PAGE * DV], I32, name="vw_pool", offset=VW_POOL_AT)
+        nc.scalar.dma_start(
+            vw_pool[:].rearrange("p (u e) -> p u e", e=DV),
+            v_words.rearrange("u p e r -> p u (e r)").bitcast(I32),
+        )
         gather_keys(2)
         row_max(0, 0)
         row_max(1, 0)
@@ -267,14 +274,13 @@ def tile_attend_pkv8_sink_kernel(tc, qT, k_words, k_scales, v_words, v_scales, v
         score(3, 0)
         row_max(1, 1)
         exponentiate(1)
-        turn(0, 0)
-        turn(0, 1)
-        row_max(2, 0)
         gather_keys(3)
         score(2, 1)
         score(3, 1)
+        turn(0, 0)
+        turn(0, 1)
         scale_planes(0, 0)
-        scale_planes(0, 1)
+        row_max(2, 0)
         row_max(3, 0)
         row_max(2, 1)
         turn(1, 0)
@@ -287,7 +293,6 @@ def tile_attend_pkv8_sink_kernel(tc, qT, k_words, k_scales, v_words, v_scales, v
         turn(3, 0)
         turn(3, 1)
         weave(0, 0)
-        weave(0, 1)
         scale_planes(2, 0)
         scale_planes(2, 1)
         weave(2, 0)
@@ -297,6 +302,7 @@ def tile_attend_pkv8_sink_kernel(tc, qT, k_words, k_scales, v_words, v_scales, v
         vw = turns.tile([P, B * PAGES * DV], U32, name="vw", align_bytes=64, offset=KW_AT[3] + 1024)
         nc.vector.tensor_copy(vw[:], vw_pool[:].bitcast(U32).indirect(voffsets[:]))
         inverse = keep.tile([P, TILES], F32, name="inverse")
+        weigh(0, 1)
         weigh(1, 0)
         weigh(1, 1)
         quantize_w(0, 0, 2)

@@ -26,24 +26,30 @@ ROW = N + PACK
 PLANE = 264
 VS_ROW = P - 1
 V_PLANE = 4
+VS_SEED = 8
+QUAD = 32
+SINK_STEP = QUAD // TILES
 SCORE_BANK = {(c, e): 2 * c + e for c in range(TILES) for e in range(PAGES)}
 SUM_BANK = (4, 5, 0, 1)
-SINK_ROW = P - TILES
 FILL = -(2.0**120)
 
 VS_AT = 0
-Q0_CODES_AT = 83968
+Q0_CODES_AT = VS_AT
 Q0_RAW_AT = 86016
 KS_ROW = P - 16
-VS_EARLY = 2816
-SINK_AT = 102400
+VS_EARLY = 2176
+Q_BF_AT = 106496
+VSC_POOL_AT = Q0_RAW_AT
 KS_AT = 16384
-VW_POOL_AT = 75776
 KW_POOL_AT = 20480
 NEG_AT = 36864
 NEG_BYTES = 4224
 PROB_AT = NEG_AT + TILES * NEG_BYTES
-KW_AT = (74752, 70656, 72704, 70656)
+Q1_RAW_AT = KS_AT
+KW_AT = (74752, 70656, 72704, Q1_RAW_AT + 2048)
+VW_POOL_AT = Q1_RAW_AT - 7168
+VSC_AT = KW_AT[3] - 512
+VW_AT = KW_AT[3] + 512
 
 
 def tile_attend_pkv8_sink_kernel(tc, qT, k_words, k_scales, v_words, v_scales, vs, sink, offs, voffs, out):
@@ -57,36 +63,41 @@ def tile_attend_pkv8_sink_kernel(tc, qT, k_words, k_scales, v_words, v_scales, v
         voffsets = keep.tile([P, B * PAGES * DV // 16], U16, name="voffsets")
         ks_pool = turns.tile([P, T // 4], I32, name="ks_pool", offset=KS_AT)
         vs_pool = turns.tile([P, T], F32, name="vs_pool", offset=VS_AT)
-        sink_rows = turns.tile([P, P], F32, name="sink_rows", offset=SINK_AT)
+        vs_seed = keep.tile([P, VS_SEED], F32, name="vs_seed")
+        sink_rows = keep.tile([P, QUAD], F32, name="sink_rows", align_bytes=64)
+        ident = keep.tile([P, P], F32, name="ident")
+        nc.vector.memset(ident[:], 0.0)
+        make_identity(nc, ident[:], nomemset=True)
+        nc.vector.memset(sink_rows[:], FILL)
         nc.vector.memset(ks_pool[0:KS_ROW, :], 0)
         ks = keep.tile([P, B * N], U8, name="ks", align_bytes=64)
         nc.vector.memset(ks[:].bitcast(I32), 0)
         nc.vector.memset(vs_pool[0:VS_ROW, 0:VS_EARLY], 0.0)
-        nc.gpsimd.memset(sink_rows[0:SINK_ROW, :], FILL)
 
-        q_raw = [turns.tile([P, PACK, NQ], F32, name="q_raw%d" % b, offset=Q0_RAW_AT + 8192 * b) for b in range(B)]
+        q_raw = {0: turns.tile([P, PACK, NQ], F32, name="q_raw0", offset=Q0_RAW_AT)}
         kw_pool = turns.tile([P, T], I32, name="kw_pool", offset=KW_POOL_AT)
         nc.sync.dma_start(offsets[:], offs)
         nc.sync.dma_start(ks_pool[KS_ROW:P, :], k_scales[0].bitcast(I32))
-        nc.sync.dma_start(q_raw[0][:], qT[0].rearrange("(p j) q -> p j q", j=PACK))
-        nc.sync.dma_start(sink_rows[SINK_ROW:P, :], sink.rearrange("b (h p) o -> (b h) (p o)", p=P))
+        nc.sync.dma_start(vs_seed[:], vs[:, 0:VS_SEED])
+        nc.sync.dma_start(sink_rows[0:P:SINK_STEP, :], sink.rearrange("b (h u j) o -> u (b h) (j o)", h=HALVES, j=QUAD))
         nc.sync.dma_start(vs_pool[VS_ROW:P, :], vs[0:1, :])
+        nc.sync.dma_start(q_raw[0][:], qT[0].rearrange("(p j) q -> p j q", j=PACK))
         nc.sync.dma_start(kw_pool[:], k_words[0].rearrange("p t r -> p (t r)").bitcast(I32))
-        nc.sync.dma_start(q_raw[1][:], qT[1].rearrange("(p j) q -> p j q", j=PACK))
         nc.sync.dma_start(voffsets[:], voffs)
 
         neg = [turns.tile([P, ROW], F32, name="neg%d" % c, offset=NEG_AT + c * NEG_BYTES) for c in range(TILES)]
 
         ks_rows = keep.tile([P, B * N], U8, name="ks_rows", align_bytes=64)
         nc.vector.tensor_copy(ks_rows[:], ks_pool[:].bitcast(U8).indirect(offsets[:]))
-        nc.vector.memset(vs_pool[0:VS_ROW, VS_EARLY:T], 0.0)
+        sink_cols = keep.tile([P, QUAD], F32, name="sink_cols", align_bytes=64)
+        nc.vector.transpose(sink_cols[:], sink_rows[:])
 
         q_bf = {}
         q_codes = {}
         q_scales = [keep.tile([P, NQ], U8, name="q_scales%d" % b, align_bytes=64) for b in range(B)]
 
         def cast_q(b):
-            q_bf[b] = turns.tile([P, NQ, PACK], BF16, name="q_bf%d" % b, align_bytes=64, offset=(SINK_AT + 2048, SINK_AT)[b])
+            q_bf[b] = turns.tile([P, NQ, PACK], BF16, name="q_bf%d" % b, align_bytes=64, offset=(Q_BF_AT + 2048, Q_BF_AT)[b])
             nc.scalar.copy(
                 out=q_bf[b][:].rearrange("p (c i) j -> p c j i", i=4),
                 in_=q_raw[b][:].rearrange("p j (c i) -> p c j i", i=4),
@@ -100,21 +111,23 @@ def tile_attend_pkv8_sink_kernel(tc, qT, k_words, k_scales, v_words, v_scales, v
                 in_=q_bf[b][:].rearrange("p q j -> p (q j)"),
             )
 
-        cast_q(0)
-        quantize_q(0)
-
-        ident = turns.tile([P, P], F32, name="ident", offset=Q0_RAW_AT + 2048)
-        make_identity(nc, ident[:])
-        for c in range(TILES):
-            sink_bank = psum.tile([P, P], F32, name="sink_bank", tag="bank%d" % c)
-            nc.tensor.transpose(sink_bank[:], sink_rows[:], ident[:])
-            nc.scalar.activation(out=neg[c][:, N:ROW], in_=sink_bank[:, SINK_ROW + c - 3 * TILES : P : TILES], func=ACT.Copy, scale=-1.0)
-
+        nc.scalar.activation(
+            out=vs_pool[0:VS_ROW, VS_EARLY:T].rearrange("p (r s) -> p r s", s=VS_SEED),
+            in_=vs_seed[0:VS_ROW, :].unsqueeze(1).to_broadcast([VS_ROW, (T - VS_EARLY) // VS_SEED, VS_SEED]),
+            func=ACT.Copy,
+        )
         for r in range(4):
-            nc.scalar.dma_start(ks[r:P:32, :].bitcast(I32), ks_rows[KS_ROW + r : P : 4, :].bitcast(I32))
+            nc.sync.dma_start(ks[r:P:32, :].bitcast(I32), ks_rows[KS_ROW + r : P : 4, :].bitcast(I32))
+        q_raw[1] = turns.tile([P, PACK, NQ], F32, name="q_raw1", offset=Q1_RAW_AT)
+        nc.sync.dma_start(q_raw[1][:], qT[1].rearrange("(p j) q -> p j q", j=PACK))
+        cast_q(0)
+
+        for c in range(TILES):
+            nc.scalar.activation(out=neg[c][:, N:ROW], in_=sink_cols[:, c * SINK_STEP : c * SINK_STEP + PACK], func=ACT.Copy, scale=-1.0)
 
         vs_slots = keep.tile([P, B * N], F32, name="vs_slots")
         nc.vector.tensor_copy(vs_slots[:], vs_pool[:].indirect(offsets[:]))
+        quantize_q(0)
         vs_cols = keep.tile([P, B * PAGES, 2 * PACK], F32, name="vs_cols")
         for g in range(B * PAGES):
             nc.sync.dma_start(
@@ -122,8 +135,8 @@ def tile_attend_pkv8_sink_kernel(tc, qT, k_words, k_scales, v_words, v_scales, v
                 vs_slots[VS_ROW:P, g * PAGE : (g + 1) * PAGE].rearrange("o (p t) -> o p t", t=PACK),
             )
 
-        vsc_pool = turns.tile([P, T // PAGE * DV // 4], I32, name="vsc_pool", offset=Q0_RAW_AT + 2560)
-        nc.gpsimd.memset(vsc_pool[:], 0)
+        vsc_pool = turns.tile([P, T // PAGE * DV // 4], I32, name="vsc_pool", offset=VSC_POOL_AT)
+        nc.vector.memset(vsc_pool[:], 0)
         for r in range(4):
             nc.sync.dma_start(
                 vsc_pool[V_PLANE + r : P : 32, :].rearrange("f (u e) -> f u e", u=T // PAGE),
@@ -167,7 +180,7 @@ def tile_attend_pkv8_sink_kernel(tc, qT, k_words, k_scales, v_words, v_scales, v
             scores[c, e] = bank
 
         def row_max(c, e):
-            first = neg[c][:, ROW - 1 : ROW] if e == 0 else neg_max[c // HALVES][:, c % HALVES, e - 1 : e]
+            first = neg[c][:, N : N + 1] if e == 0 else neg_max[c // HALVES][:, c % HALVES, e - 1 : e]
             nc.vector.tensor_scalar(
                 out=neg[c][:, e * PAGE : (e + 1) * PAGE],
                 in0=scores[c, e][:],
@@ -297,9 +310,9 @@ def tile_attend_pkv8_sink_kernel(tc, qT, k_words, k_scales, v_words, v_scales, v
         scale_planes(2, 1)
         weave(2, 0)
         weave(2, 1)
-        vsc = turns.tile([P, B * PAGES * DV], U8, name="vsc", align_bytes=64, offset=KW_AT[3])
+        vsc = turns.tile([P, B * PAGES * DV], U8, name="vsc", align_bytes=64, offset=VSC_AT)
         nc.vector.tensor_copy(vsc[:], vsc_pool[:].bitcast(U8).indirect(voffsets[:]))
-        vw = turns.tile([P, B * PAGES * DV], U32, name="vw", align_bytes=64, offset=KW_AT[3] + 1024)
+        vw = turns.tile([P, B * PAGES * DV], U32, name="vw", align_bytes=64, offset=VW_AT)
         nc.vector.tensor_copy(vw[:], vw_pool[:].bitcast(U32).indirect(voffsets[:]))
         inverse = keep.tile([P, TILES], F32, name="inverse")
         weigh(0, 1)

from contextlib import ExitStack

import concourse.mybir as mybir
from concourse.masks import make_identity

B, N, T, D, DV, NQ = 2, 1024, 4096, 512, 256, 256
PAGE = 512
FLOPS = 2 * B * NQ * N * (D + DV)

F32 = mybir.dt.float32
BF16 = mybir.dt.bfloat16
I32 = mybir.dt.int32
U32 = mybir.dt.uint32
U16 = mybir.dt.uint16
U8 = mybir.dt.uint8
FP8X4 = mybir.dt.float8_e4m3fn_x4
ALU = mybir.AluOpType
ACT = mybir.ActivationFunctionType

P = 128
PACK = 4
PAGES = N // PAGE
TILES = B * NQ // P
HALVES = NQ // P
ROW = N + PACK
PLANE = 264
VS_ROW = P - 1
V_PLANE = 4
VS_SEED = 8
QUAD = 32
SINK_STEP = QUAD // TILES
SCORE_BANK = {(c, e): 2 * c + e for c in range(TILES) for e in range(PAGES)}
SUM_BANK = (4, 5, 0, 1)
FILL = -(2.0**120)

VS_AT = 0
Q0_CODES_AT = VS_AT
Q0_RAW_AT = 86016
KS_ROW = P - 16
VS_EARLY = 2176
Q_BF_AT = 106496
VSC_POOL_AT = Q0_RAW_AT
KS_AT = 16384
KW_POOL_AT = 20480
NEG_AT = 36864
NEG_BYTES = 4224
PROB_AT = NEG_AT + TILES * NEG_BYTES
Q1_RAW_AT = KS_AT
KW_AT = (74752, 70656, 72704, Q1_RAW_AT + 2048)
VW_POOL_AT = Q1_RAW_AT - 7168
VSC_AT = KW_AT[3] - 512
VW_AT = KW_AT[3] + 512


def tile_attend_pkv8_sink_kernel(tc, qT, k_words, k_scales, v_words, v_scales, vs, sink, offs, voffs, out):
    nc = tc.nc
    with ExitStack() as ctx:
        keep = ctx.enter_context(tc.tile_pool(name="keep", bufs=1))
        turns = ctx.enter_context(tc.tile_pool(name="turns", bufs=1))
        psum = ctx.enter_context(tc.psum_pool(name="psum", bufs=1))

        offsets = keep.tile([P, B * N // 16], U16, name="offsets")
        voffsets = keep.tile([P, B * PAGES * DV // 16], U16, name="voffsets")
        ks_pool = turns.tile([P, T // 4], I32, name="ks_pool", offset=KS_AT)
        vs_pool = turns.tile([P, T], F32, name="vs_pool", offset=VS_AT)
        vs_seed = keep.tile([P, VS_SEED], F32, name="vs_seed")
        sink_rows = keep.tile([P, QUAD], F32, name="sink_rows", align_bytes=64)
        ident = keep.tile([P, P], F32, name="ident")
        nc.vector.memset(ident[:], 0.0)
        make_identity(nc, ident[:], nomemset=True)
        nc.vector.memset(sink_rows[:], FILL)
        nc.vector.memset(ks_pool[0:KS_ROW, :], 0)
        ks = keep.tile([P, B * N], U8, name="ks", align_bytes=64)
        nc.vector.memset(ks[:].bitcast(I32), 0)
        nc.vector.memset(vs_pool[0:VS_ROW, 0:VS_EARLY], 0.0)

        q_raw = {0: turns.tile([P, PACK, NQ], F32, name="q_raw0", offset=Q0_RAW_AT)}
        kw_pool = turns.tile([P, T], I32, name="kw_pool", offset=KW_POOL_AT)
        nc.sync.dma_start(offsets[:], offs)
        nc.sync.dma_start(ks_pool[KS_ROW:P, :], k_scales[0].bitcast(I32))
        nc.sync.dma_start(vs_seed[:], vs[:, 0:VS_SEED])
        nc.sync.dma_start(sink_rows[0:P:SINK_STEP, :], sink.rearrange("b (h u j) o -> u (b h) (j o)", h=HALVES, j=QUAD))
        nc.sync.dma_start(vs_pool[VS_ROW:P, :], vs[0:1, :])
        nc.sync.dma_start(q_raw[0][:], qT[0].rearrange("(p j) q -> p j q", j=PACK))
        nc.sync.dma_start(kw_pool[:], k_words[0].rearrange("p t r -> p (t r)").bitcast(I32))
        nc.sync.dma_start(voffsets[:], voffs)

        neg = [turns.tile([P, ROW], F32, name="neg%d" % c, offset=NEG_AT + c * NEG_BYTES) for c in range(TILES)]

        ks_rows = keep.tile([P, B * N], U8, name="ks_rows", align_bytes=64)
        nc.vector.tensor_copy(ks_rows[:], ks_pool[:].bitcast(U8).indirect(offsets[:]))
        sink_cols = keep.tile([P, QUAD], F32, name="sink_cols", align_bytes=64)
        nc.vector.transpose(sink_cols[:], sink_rows[:])

        q_bf = {}
        q_codes = {}
        q_scales = [keep.tile([P, NQ], U8, name="q_scales%d" % b, align_bytes=64) for b in range(B)]

        def cast_q(b):
            q_bf[b] = turns.tile([P, NQ, PACK], BF16, name="q_bf%d" % b, align_bytes=64, offset=(Q_BF_AT + 2048, Q_BF_AT)[b])
            nc.scalar.copy(
                out=q_bf[b][:].rearrange("p (c i) j -> p c j i", i=4),
                in_=q_raw[b][:].rearrange("p j (c i) -> p c j i", i=4),
            )

        def quantize_q(b):
            q_codes[b] = turns.tile([P, NQ], U32, name="q_codes%d" % b, align_bytes=64, offset=(Q0_CODES_AT, KW_AT[0])[b])
            nc.vector.quantize_mx(
                out=q_codes[b][:].bitcast(FP8X4),
                scales=q_scales[b][:],
                in_=q_bf[b][:].rearrange("p q j -> p (q j)"),
            )

        nc.scalar.activation(
            out=vs_pool[0:VS_ROW, VS_EARLY:T].rearrange("p (r s) -> p r s", s=VS_SEED),
            in_=vs_seed[0:VS_ROW, :].unsqueeze(1).to_broadcast([VS_ROW, (T - VS_EARLY) // VS_SEED, VS_SEED]),
            func=ACT.Copy,
        )
        for r in range(4):
            nc.sync.dma_start(ks[r:P:32, :].bitcast(I32), ks_rows[KS_ROW + r : P : 4, :].bitcast(I32))
        q_raw[1] = turns.tile([P, PACK, NQ], F32, name="q_raw1", offset=Q1_RAW_AT)
        nc.sync.dma_start(q_raw[1][:], qT[1].rearrange("(p j) q -> p j q", j=PACK))
        cast_q(0)

        for c in range(TILES):
            nc.scalar.activation(out=neg[c][:, N:ROW], in_=sink_cols[:, c * SINK_STEP : c * SINK_STEP + PACK], func=ACT.Copy, scale=-1.0)

        vs_slots = keep.tile([P, B * N], F32, name="vs_slots")
        nc.vector.tensor_copy(vs_slots[:], vs_pool[:].indirect(offsets[:]))
        quantize_q(0)
        vs_cols = keep.tile([P, B * PAGES, 2 * PACK], F32, name="vs_cols")
        for g in range(B * PAGES):
            nc.sync.dma_start(
                vs_cols[:, g, 0:PACK],
                vs_slots[VS_ROW:P, g * PAGE : (g + 1) * PAGE].rearrange("o (p t) -> o p t", t=PACK),
            )

        vsc_pool = turns.tile([P, T // PAGE * DV // 4], I32, name="vsc_pool", offset=VSC_POOL_AT)
        nc.vector.memset(vsc_pool[:], 0)
        for r in range(4):
            nc.sync.dma_start(
                vsc_pool[V_PLANE + r : P : 32, :].rearrange("f (u e) -> f u e", u=T // PAGE),
                v_scales[:, r:16:4, :].rearrange("u f e -> f u e").bitcast(I32),
            )

        cast_q(1)

        kw = {}
        neg_max = [keep.tile([P, HALVES, PAGES], F32, name="neg_max%d" % b) for b in range(B)]
        total = keep.tile([P, TILES], F32, name="total")
        prob = {}
        w_bf = {c: keep.tile([P, PAGES, P, PACK], BF16, name="w_bf%d" % c, align_bytes=64) for c in range(TILES)}
        w_codes = {c: keep.tile([P, PAGES, P], U32, name="w_codes%d" % c, align_bytes=64) for c in range(TILES) if c != 1}
        w_scales = [keep.tile([P, PAGES, P], U8, name="w_scales%d" % c, align_bytes=64) for c in range(TILES)]
        scores = {}
        turned = {}
        sums = {}
        planes = {}

        def gather_keys(g):
            kw[g] = turns.tile([P, PAGE], U32, name="kw%d" % g, align_bytes=64, offset=KW_AT[g])
            nc.vector.tensor_copy(
                kw[g][:],
                kw_pool[:].bitcast(U32).indirect(offsets[:, g * PAGE // 16 : (g + 1) * PAGE // 16]),
            )

        def score(c, e):
            b, h = divmod(c, HALVES)
            g = b * PAGES + e
            bank = psum.tile([P, PAGE], F32, name="scores", tag="bank%d" % SCORE_BANK[c, e])
            nc.tensor.matmul_mx(
                out=bank[:],
                lhsT=q_codes[b][:, h * P : (h + 1) * P].bitcast(FP8X4),
                lhsT_scale=q_scales[b][:, h * P : (h + 1) * P],
                rhs=kw[g][:].bitcast(FP8X4),
                rhs_scale=ks[:, g * PAGE : (g + 1) * PAGE],
                start=True,
                stop=True,
            )
            scores[c, e] = bank

        def row_max(c, e):
            first = neg[c][:, N : N + 1] if e == 0 else neg_max[c // HALVES][:, c % HALVES, e - 1 : e]
            nc.vector.tensor_scalar(
                out=neg[c][:, e * PAGE : (e + 1) * PAGE],
                in0=scores[c, e][:],
                scalar1=-1.0,
                scalar2=first,
                op0=ALU.mult,
                op1=ALU.min,
                accum_out=neg_max[c // HALVES][:, c % HALVES, e : e + 1],
            )

        def exponentiate(c):
            prob[c] = turns.tile([P, PACK, PLANE], F32, name="prob%d" % c, offset=PROB_AT + c * NEG_BYTES)
            nc.scalar.activation(
                out=prob[c][:, :, 0 : ROW // PACK].rearrange("p t s -> p s t"),
                in_=neg[c][:].rearrange("p (s t) -> p s t", t=PACK),
                func=ACT.Exp,
                scale=-1.0,
                bias=neg_max[c // HALVES][:, c % HALVES, PAGES - 1 : PAGES],
                accum_out=total[:, c : c + 1],
            )

        def turn(c, e):
            bank = psum.tile([P, PACK, P], F32, name="turned", tag="bank%d" % SCORE_BANK[c, e])
            for t in range(PACK):
                nc.tensor.transpose(bank[:, t, :], prob[c][:, t, e * P : (e + 1) * P], ident[:])
            turned[c, e] = bank

        def weigh(c, e):
            g = c // HALVES * PAGES + e
            nc.vector.tensor_tensor(
                out=w_bf[c][:, e, :, :],
                in0=turned[c, e][:].rearrange("p t q -> p q t"),
                in1=vs_cols[:, g, 0:PACK].unsqueeze(1).to_broadcast([P, P, PACK]),
                op=ALU.mult,
            )

        def scale_planes(c, e):
            g = c // HALVES * PAGES + e
            planes[c, e] = keep.tile([P, PACK, P], BF16, name="planes%d_%d" % (c, e))
            for t in range(PACK):
                nc.scalar.activation(
                    out=planes[c, e][:, t, :],
                    in_=turned[c, e][:, t, :],
                    func=ACT.Copy,
                    scale=vs_cols[:, g, t : t + 1],
                )

        def weave(c, e):
            nc.scalar.copy(
                out=w_bf[c][:, e, :, :].rearrange("p (k i) t -> p k t i", i=4),
                in_=planes[c, e][:].rearrange("p t (k i) -> p k t i", i=4),
            )

        def quantize_w(c, e0, e1):
            nc.vector.quantize_mx(
                out=w_codes[c][:, e0:e1, :].rearrange("p e q -> p (e q)").bitcast(FP8X4),
                scales=w_scales[c][:, e0:e1, :].rearrange("p e q -> p (e q)"),
                in_=w_bf[c][:, e0:e1, :, :].rearrange("p e q t -> p (e q t)"),
            )

        def multiply(c, e, first):
            g = c // HALVES * PAGES + e
            if first:
                sums[c] = psum.tile([P, DV], F32, name="sums", tag="bank%d" % SUM_BANK[c])
            nc.tensor.matmul_mx(
                out=sums[c][:],
                lhsT=w_codes[c][:, e, :].bitcast(FP8X4),
                lhsT_scale=w_scales[c][:, e, :],
                rhs=vw[:, g * DV : (g + 1) * DV].bitcast(FP8X4),
                rhs_scale=vsc[V_PLANE:P, g * DV : (g + 1) * DV],
                start=first,
                stop=not first,
            )

        def finish(c):
            b, h = divmod(c, HALVES)
            y = keep.tile([P, DV], F32, name="y%d" % c)
            if c != TILES - 1:
                nc.scalar.activation(out=y[:], in_=sums[c][:], func=ACT.Copy, scale=inverse[:, c : c + 1])
            else:
                nc.vector.tensor_scalar(
                    out=y[:], in0=sums[c][:], scalar1=inverse[:, c : c + 1], scalar2=None, op0=ALU.mult
                )
            nc.sync.dma_start(out[b, h * P : (h + 1) * P, :], y[:])

        gather_keys(0)
        score(0, 0)
        score(1, 0)
        gather_keys(1)
        score(0, 1)
        score(1, 1)
        vw_pool = turns.tile([P, T // PAGE * DV], I32, name="vw_pool", offset=VW_POOL_AT)
        nc.scalar.dma_start(
            vw_pool[:].rearrange("p (u e) -> p u e", e=DV),
            v_words.rearrange("u p e r -> p u (e r)").bitcast(I32),
        )
        gather_keys(2)
        row_max(0, 0)
        row_max(1, 0)
        row_max(0, 1)
        exponentiate(0)
        quantize_q(1)
        score(2, 0)
        score(3, 0)
        row_max(1, 1)
        exponentiate(1)
        gather_keys(3)
        score(2, 1)
        score(3, 1)
        turn(0, 0)
        turn(0, 1)
        scale_planes(0, 0)
        row_max(2, 0)
        row_max(3, 0)
        row_max(2, 1)
        turn(1, 0)
        turn(1, 1)
        exponentiate(2)
        row_max(3, 1)
        exponentiate(3)
        turn(2, 0)
        turn(2, 1)
        turn(3, 0)
        turn(3, 1)
        weave(0, 0)
        scale_planes(2, 0)
        scale_planes(2, 1)
        weave(2, 0)
        weave(2, 1)
        vsc = turns.tile([P, B * PAGES * DV], U8, name="vsc", align_bytes=64, offset=VSC_AT)
        nc.vector.tensor_copy(vsc[:], vsc_pool[:].bitcast(U8).indirect(voffsets[:]))
        vw = turns.tile([P, B * PAGES * DV], U32, name="vw", align_bytes=64, offset=VW_AT)
        nc.vector.tensor_copy(vw[:], vw_pool[:].bitcast(U32).indirect(voffsets[:]))
        inverse = keep.tile([P, TILES], F32, name="inverse")
        weigh(0, 1)
        weigh(1, 0)
        weigh(1, 1)
        quantize_w(0, 0, 2)
        multiply(0, 0, True)
        multiply(0, 1, False)
        nc.vector.reciprocal(out=inverse[:], in_=total[:])
        weigh(3, 0)
        w_codes[1] = turns.tile([P, PAGES, P], U32, name="w_codes1", align_bytes=64, offset=PROB_AT + 3 * NEG_BYTES)
        quantize_w(1, 0, 2)
        multiply(1, 0, True)
        multiply(1, 1, False)
        finish(0)
        finish(1)
        quantize_w(3, 0, 1)
        multiply(3, 0, True)
        quantize_w(2, 0, 1)
        multiply(2, 0, True)
        weigh(3, 1)
        quantize_w(2, 1, 2)
        quantize_w(3, 1, 2)
        multiply(2, 1, False)
        multiply(3, 1, False)
        finish(2)
        finish(3)
